import numpy as np, ml_dtypes
CORES = [36,164,52,180,100,228,116,244]
N = 8
import mx_ref
BF = ml_dtypes.bfloat16
def gentries(a):
    return np.ascontiguousarray(a.reshape(8, 16, -1).transpose(0, 2, 1)).reshape(8, -1)
def gtable(e):
    e = np.asarray(e); return np.ascontiguousarray(e.reshape(8, -1, 16).transpose(0, 2, 1)).reshape(128, -1).astype(np.int32)
def gcols(t, e):
    v = np.concatenate([t.reshape(8, 16, -1, 4), np.zeros((8, 16, 1, 4), BF)], axis=2)
    return np.ascontiguousarray(np.stack([v[g][:, e[g]] for g in range(8)])).reshape(128, -1)
def tile(rs):
    return np.stack(rs, axis=2).reshape(128, -1).astype(BF)
def cut(t, i, w=512):
    return t[:, w * i:w * i + w]
def pick(q, e):
    c = np.concatenate([q[0].reshape(128, -1, 4), np.zeros((128, 1, 4), np.uint8)], axis=1); s = np.concatenate([q[1], np.ones((16, 1), np.uint8)], axis=1)
    return (np.ascontiguousarray(c[:, e].reshape(128, -1)), np.ascontiguousarray(s[:, e]))
def join(*qs):
    return (np.concatenate([q[0] for q in qs], axis=1), np.concatenate([q[1] for q in qs], axis=1))
def put(q, e, v):
    c, s = q[0].reshape(128, -1, 4).copy(), q[1].copy(); c[:, e] = v[0].reshape(128, -1, 4); s[:, e] = v[1]
    return (c.reshape(128, -1), s)
def pk(c, s):
    return (np.ascontiguousarray(c), mx_ref.live(s))
def emit(q):
    return q[0], q[1]
def packed(v, rng):
    q = [mx_ref.quantize(np.ascontiguousarray(v[r])) for r in range(N)]
    return np.stack([a for a, b in q]), np.stack([mx_ref.plane(b, rng) for a, b in q])
def values_of_codes():
    e, c = np.zeros((128, 128, 4), np.float32), np.zeros((128, 2, 4), np.uint8)
    e[np.arange(128), np.arange(128), 0] = 1
    c[:127, :, 0] = np.arange(256).reshape(2, 128).T[:127]
    return mx_ref.matmul(mx_ref.quantize(e.reshape(128, 512).astype(BF)), (c.reshape(128, 8), np.full((16, 2), 127, np.uint8))).T.reshape(-1).astype(np.float64)
CODE_VALUE, SCALE_VALUE = values_of_codes(), 2.0 ** (np.arange(256) - 127.0)
def decode(q):
    return (CODE_VALUE[q[0]].reshape(16, 8, -1, 4) * SCALE_VALUE[q[1]][:, None, :, None] + 0.0).reshape(128, -1).astype(np.float32)
def f(rng, *shape):
    return mx_ref.flush((rng.standard_normal(shape, dtype=np.float32) * np.exp2(rng.integers(-2, 3, shape[:-1] + (1,)))).astype(BF))
def wide(rng, *shape, cols=0):
    v = rng.standard_normal(shape, dtype=np.float32) * np.exp2(rng.integers(-12, 13, shape)).astype(np.float32)
    if cols: v *= np.repeat(np.exp2(rng.integers(-cols, cols + 1, shape[:-2] + (1, shape[-1] // 4))) * (rng.random(shape[:-2] + (1, shape[-1] // 4)) > 0.0625), 4, axis=-1).astype(np.float32)
    return mx_ref.flush(v.astype(BF))
C, V, L, K, R = 320, 4, 4, 64, 3
def order(s, names):
    by = np.argsort(np.argsort(-s, axis=1, kind="stable"), axis=1)
    place = np.where(by == 0, 0, C)
    for t in range(L):
        first = np.min(np.take_along_axis(place, names.reshape(8, -1), axis=1).reshape(8, C, V), axis=2)
        new = (place == C) & (first < C)
        key = np.where(new, first * C + by, C * C)
        n = np.sum(place < C, axis=1)
        place = np.where(new, n[:, None] + np.argsort(np.argsort(key, axis=1, kind="stable"), axis=1), place)
    return np.argsort(place, axis=1, kind="stable")
def big(v):
    v = v.astype(np.float32)
    v[np.abs(v) < np.float32(2.0 ** -16)] = 0
    return v.astype(BF)
def numbers_of(rng):
    return {"x": big(f(rng, N, 128, 4 * C)), "u": np.array(f(rng, N, 128, 512)), "v": np.array(f(rng, N, 128, 512))}
def names_of(rng):
    return rng.integers(0, C, (N, 8, C, V))
def stored(l):
    return {"nb": np.stack([gtable(e.reshape(8, -1)) for e in l])}
def weights(rng, w):
    c, p = packed(w, rng)
    return {"wc": c, "ws": p}
def still(rng):
    w = np.zeros((N, 128, 4, 128, 4), np.float32)
    i = np.arange(128)
    for b in range(4): w[:, i, b, i, b] = 32
    return weights(rng, w.reshape(N, 128, 2048).astype(BF))
def signs(rng):
    return np.stack([rng.permutation(8) % 2 * 2.0 - 1.0 for r in range(N)])
def setup_inputs(rng):
    return {**numbers_of(rng), **stored(names_of(rng)), **weights(rng, f(rng, N, 128, 2048))}
def setup_inputs_ties(rng):
    d = numbers_of(rng)
    e = rng.permutation(N)
    x = d["x"].reshape(N, 8, 16, C, 4)
    for r in range(N):
        k = np.zeros(C, int) if r == e[0] else rng.permutation(C) % 3
        a = x[r][:, :8, :3].copy()
        a[:, :, 2] = 0
        x[r][:, :8] = a[:, :, k]
    x[e[1]] = 0
    u = d["u"].reshape(N, 8, 16, 128, 4)
    u[:, :, 8:, ::16] = 0
    w = np.array(f(rng, N, 128, 2048)).reshape(N, 8, 16, 4, 8, 16, 4)
    w[:, :, 8:, :, :, :8] = 0
    return {"x": x.reshape(N, 128, 4 * C), "u": u.reshape(N, 128, 512), "v": d["v"], **stored(names_of(rng)), **weights(rng, w.reshape(N, 128, 2048))}
def setup_inputs_near(rng):
    d, l = numbers_of(rng), names_of(rng)
    x = d["x"].astype(np.float32).reshape(N, 8, 16, C, 4)
    s = np.arange(C) // 2
    g = ((s[:, None] >> np.arange(8)) & 1) * np.exp2(np.arange(8) - 23.0)
    x[:, :, 0] = 0
    x[:, :, 0, :, 0] = 1
    x[:, :, 8] = g[:, :4]
    x[:, :, 9] = g[:, 4:]
    x[:, :, 10:] = rng.integers(4, 8, (N, 8, 6, C, 4)) * rng.choice([-1.0, 1.0], (N, 8, 6, C, 4)) * 2.0 ** -20
    u = d["u"].reshape(N, 128, 128, 4)
    k = np.where(rng.permutation(N) < N // 2, 2.0 ** -30, 1.0)
    a = k[:, None] * signs(rng)
    a[np.ix_(np.flatnonzero(k < 1), rng.permutation(8)[:2])] = 0
    a = a.astype(np.float32).astype(BF)
    k = k.astype(np.float32).astype(BF)
    u[:, :, ::16] = 0
    for h in range(0, 128, 16):
        u[:, h, h, 0] = a[:, h // 16]
        u[:, h + 8:h + 10, h] = k[:, None, None]
    l[:, :, :C // 4, 0] = C - 2
    l[:, :, 1::2] = l[:, :, ::2]
    return {"x": x.reshape(N, 128, 4 * C).astype(BF), "u": u.reshape(N, 128, 512), "v": d["v"], **stored(l), **still(rng)}
def setup_inputs_huge(rng):
    d = numbers_of(rng)
    x = 2.0 ** 30 * (0.6 + 0.4 * rng.random((N, 128, C, 4)))
    c = np.stack([rng.permutation(C) % 2 * 2.0 - 1.0 for r in range(N)])
    c[rng.permutation(N) < N // 2] = 1
    x *= c[:, None, :, None]
    u = d["u"].reshape(N, 128, 128, 4)
    a = 2.0 ** 30 * (1 - 0.25 * rng.random((N, 128, 8, 4))) * signs(rng)[:, None, :, None]
    u[:, :, ::16] = a.astype(np.float32).astype(BF)
    return {"x": x.astype(np.float32).reshape(N, 128, 4 * C).astype(BF), "u": u.reshape(N, 128, 512), "v": d["v"], **stored(names_of(rng)), **still(rng)}
def setup_inputs_graphs(rng):
    d, l = numbers_of(rng), names_of(rng)
    o = rng.permutation(N)
    x = d["x"].reshape(N, 8, 16, C, 4)
    u = d["u"].reshape(N, 128, 128, 4)
    u[:, ::16, ::16, 0] = np.eye(8, dtype=np.float32).astype(BF)
    for r in range(N):
        for g in range(8):
            e = rng.permutation(C)
            x[r, g, 0, e[0], 0] = 16384
            if o[r] % 4 == 0: l[r, g] = np.arange(C)[:, None]
            if o[r] % 4 == 1: l[r, g] = e[0]
            if o[r] % 4 == 2: l[r, g, e] = np.roll(e, 1)[:, None]
            if o[r] % 4 == 3:
                m = L if g % 2 else 2
                l[r, g] = e[m - 1 + rng.integers(0, 2, (C, V))]
                l[r, g, e[m - 1:m + 1]] = e[m - 2]
                for j in range(1, m - 1): l[r, g, e[j]] = e[j - 1]
    return {"x": x.reshape(N, 128, 4 * C), "u": u.reshape(N, 128, 512), "v": d["v"], **stored(l), **weights(rng, f(rng, N, 128, 2048))}
def setup_inputs_spread(rng):
    d = setup_inputs(rng)
    d["x"] = big(wide(rng, N, 128, 4 * C, cols=6))
    return d
def check_inputs(d):
    b = []
    for k in ("x", "u", "v"):
        a = np.abs(d[k].astype(np.float32))
        if not (np.isfinite(a).all() and ((a == 0) | (a >= 2.0 ** -30) & (a <= 2.0 ** 30)).all()): b.append("a value of " + k)
    if ((d["nb"] < 0) | (d["nb"] >= C)).any(): b.append("an entry of nb")
    if (d["wc"] % 128 == 127).any(): b.append("wc: a code that is no number")
    for r in range(N):
        a = np.abs(decode(pk(d["wc"][r], d["ws"][r])))
        if not ((a == 0) | (a >= 2.0 ** -30) & (a <= 2.0 ** 30)).all(): b.append("a number that wc and ws stand for")
    return b
def reference(x, u, v, nb, wc, ws):
    qu = [mx_ref.quantize(u[r]) for r in range(N)]
    lay = [pk(wc[r], ws[r]) for r in range(N)]
    now = [x[r] for r in range(N)]
    names = [gentries(nb[r]).astype(np.int64).reshape(8, C, V) for r in range(N)]
    for t in range(R):
        sent = []
        for r in range(N):
            p = mx_ref.matmul(qu[r], mx_ref.quantize(now[r]))
            l = order(p[::16] + np.float32(0.0), names[r])[:, ::-1]
            i = np.argsort(l, axis=1)
            sent.append(mx_ref.quantize(gcols(now[r], l)))
            e = np.take_along_axis(names[r], l[:, :, None], axis=1).reshape(8, -1)
            names[r] = np.take_along_axis(i, e, axis=1).reshape(8, C, V)
        came = decode(join(*sent))
        for r in range(N):
            e = np.concatenate([cut(came, (r + N - 1) % N, 4 * C)[:, 4 * (C - K):], cut(came, r, 4 * C)], axis=1)
            q = mx_ref.quantize(np.ascontiguousarray(((e[:, 4 * K:] + e[:, :4 * C]) * np.float32(0.5)).astype(BF)))
            now[r] = tile([np.maximum(mx_ref.matmul(pick(lay[r], np.arange(128 * b, 128 * b + 128)), q), np.float32(0.0)) * np.float32(0.03125) for b in range(4)])
    y, on = np.zeros((N, 128, C), np.float32), np.zeros((N, 8, V * C), np.float32)
    oc, osc = np.zeros((N, 128, 4 * C), np.uint8), np.zeros((N, 16, C), np.uint8)
    for r in range(N):
        q = mx_ref.quantize(now[r])
        y[r] = mx_ref.matmul(mx_ref.quantize(v[r]), q)
        on[r] = names[r].reshape(8, -1)
        oc[r], osc[r] = emit(q)
    return {"y": y, "on": on, "oc": oc, "osc": osc}

@@ -1,0 +1,488 @@
+from concourse.mybir import dt, AluOpType, ActivationFunctionType
+
+C, KB, ROUNDS = 320, 64, 3
+NA = 12
+ND = 20 - NA
+SPLIT = 10
+BIG = 1e28
+P60 = 2.0 ** 60
+SH = 320.0 * 52428
+U3 = 131072
+F32, BF, I32, U16, Q4, U8 = "float32", "bfloat16", "int32", "uint16", "float8_e4m3fn_x4", "uint8"
+CH = (320, 192, 0)
+
+_S = {
+    "XS": (BF, 4 * C), "ZS": (BF, 4 * 384), "TT": (BF, 4 * 384), "QX": (Q4, C), "SX": (U8, C),
+    "QZ": (Q4, 384), "SZ": (U8, 384), "QW": (Q4, 512), "SW": (U8, 512),
+    "Ub": (BF, 512), "QU": (Q4, 128), "SU": (U8, 128), "QU2": (Q4, 128), "SU2": (U8, 128),
+    "Vb": (BF, 512), "QV": (Q4, 128), "SV": (U8, 128),
+    "ONE": (BF, 512), "BL1": (BF, 512), "BL2": (BF, 512), "QB": (Q4, 128), "SB": (U8, 128),
+    "EB": (BF, 2048), "QE": (Q4, 512), "SE": (U8, 512),
+    "NBI": (I32, 80), "NQ": (F32, 80), "NQI": (I32, 80), "NQ2": (F32, 80), "POS": (F32, 80),
+    "N1": (U16, 80), "N5": (U16, 80), "NALL": (F32, 100), "M5": (F32, 100), "EQ": (F32, 100), "EQS": (F32, 100),
+    "PI": (I32, 8), "CI": (I32, 8), "CF": (F32, 8), "O16I": (I32, 8), "O16": (U16, 8), "ORR": (U16, 20),
+    "I16": (F32, 16), "D16": (F32, 16), "W16": (F32, 96),
+    "M16": (F32, 20), "M4": (F32, 20), "CNT": (F32, 20), "C0": (F32, 20),
+    "T16B": (BF, C), "HH": (F32, C), "LM": (F32, C), "A3": (F32, C), "ONEF": (F32, C), "AR": (BF, 384), "APS": (BF, C * ND),
+    "TM1": (F32, 336), "T3": (F32, 640), "T4": (F32, C), "I2K": (F32, C),
+    "M3": (F32, C), "H3": (F32, C), "RD": (BF, C), "CA": (BF, 4 * 448), "CB": (BF, 4 * 256), "CC": (BF, 4 * C),
+    "QCA": (Q4, 448), "SCA": (U8, 448), "QCB": (Q4, 256), "SCB": (U8, 256), "QCC": (Q4, C), "SCC": (U8, C),
+    "RO": (BF, 4 * 384), "SG": (BF, 7 * C), "RS": (F32, 20), "UT": (F32, 20), "UO": (U16, 20),
+    "CS": (F32, C), "BYK": (F32, C), "AA": (F32, 1616), "ST": (F32, C), "O1": (U16, 20), "K1": (F32, C),
+    "G2": (F32, 1600), "G3": (F32, 1600), "G4": (F32, 1600), "K2": (F32, 1600), "K3": (F32, 1600), "K4": (F32, 1600),
+    "HOR": (F32, C), "JK": (BF, C * NA), "CMP": (BF, C * ND), "CMS": (BF, C * ND), "PL": (F32, 20),
+    "Y1": (F32, 20), "T2": (F32, 20), "C2": (F32, 20), "PM": (F32, 20), "O2": (U16, 20), "CAP": (F32, C),
+    "CW": (U16, 80),
+    "C4": (F32, C), "C4L": (F32, C), "LR": (F32, C), "HL": (F32, C), "OT": (U16, 80), "VI": (I32, 20), "LO": (I32, 20),
+    "HI": (I32, 20), "OP": (U16, 20), "CN": (F32, C), "RR": (F32, 4 * C), "ONB": (F32, 4 * C), "YS": (F32, C),
+}
+for _r in range(ROUNDS):
+    _S["QT%d" % _r] = (Q4, 448)
+    _S["STT%d" % _r] = (U8, 448)
+SCRATCH = {k: ("sbuf", [128, v[1]], v[0]) for k, v in _S.items()}
+for _b in range(8):
+    SCRATCH["ps%d" % _b] = ("psum", [128, 512], F32)
+NDMA = 16
+SEMAPHORES = ["qv", "qa", "qp", "qg", "sent"] + ["arr%d" % r for r in range(ROUNDS)] + ["d%d" % i for i in range(NDMA)]
+
+ADD, SUB, MUL, MAX, MIN = AluOpType.add, AluOpType.subtract, AluOpType.mult, AluOpType.max, AluOpType.min
+LT, LE, EQ, NE = AluOpType.is_lt, AluOpType.is_le, AluOpType.is_equal, AluOpType.not_equal
+AND, SHR = AluOpType.bitwise_and, AluOpType.arith_shift_right
+AF = ActivationFunctionType
+
+
+def rank_program(g, core, T, topo):
+    rank = T.rank_of(core)
+    if rank is None:
+        return
+    nxt = T.cores[(rank + 1) % len(T.cores)]
+    rid, pid = topo.addr(nxt, core)
+    emask = topo.mask(core, nxt)
+    neng = len(topo.engines(core, nxt))
+
+    Q = {"v": g.vector, "a": g.scalar, "p": g.tensor, "g": g, "s": g.sync}
+    count, known, clock = {}, {q: {} for q in Q}, {}
+    wr = {k: [None] * v[1] for k, v in _S.items()}
+    rd = {k: {} for k in _S}
+    bank = {"ps%d" % b: {} for b in range(8)}
+    ndma = [0]
+
+    def V(name, a=0, b=None, s=1):
+        if b is None:
+            b = 512 if name in bank else _S[name][1]
+        return (T[name][:, a:b] if s == 1 else T[name][:, a:b:s], [(name, a, b, s)])
+
+    def col(name, j):
+        return V(name, j, j + 1)
+
+    def IND(win, off):
+        return (win[0].indirect(off[0]), win[1] + off[1])
+
+    def need(q, sem, val):
+        if known[q].get(sem, 0) >= val:
+            return
+        Q[q].wait_ge(T.sem[sem], val)
+        for s2, v2 in clock.get((sem, val), {}).items():
+            if known[q].get(s2, 0) < v2:
+                known[q][s2] = v2
+        known[q][sem] = val
+
+    def op(q, call, reads, writes, dma=False, acc=False):
+        deps = {}
+
+        def dep(e):
+            if e is not None and deps.get(e[0], 0) < e[1]:
+                deps[e[0]] = e[1]
+        for n, a, b, s in reads + writes:
+            if n in bank:
+                for q2, e in bank[n].items():
+                    if q2 != q or (q == "p" and not acc):
+                        dep(e)
+        for n, a, b, s in reads:
+            if n not in bank:
+                for e in set(wr[n][a:b:s]):
+                    dep(e)
+        for n, a, b, s in writes:
+            if n not in bank:
+                for e in set(wr[n][a:b:s]):
+                    dep(e)
+                for lst in rd[n].values():
+                    for e in set(lst[a:b:s]):
+                        dep(e)
+        for sem in sorted(deps, key=lambda x: (-len(clock.get((x, deps[x]), {})), x)):
+            need(q, sem, deps[sem])
+        if dma:
+            sem, inc = "d%d" % ndma[0], 16
+            ndma[0] += 1
+        else:
+            sem, inc = "q" + q, 1
+        call().then_inc(T.sem[sem], inc)
+        count[sem] = count.get(sem, 0) + inc
+        me = (sem, count[sem])
+        clock[me] = dict(known[q])
+        for n, a, b, s in reads + writes:
+            if n in bank:
+                bank[n][q] = me
+        for n, a, b, s in reads:
+            if n not in bank:
+                lst = rd[n].setdefault(sem, [None] * _S[n][1])
+                lst[a:b:s] = [me] * len(range(a, b, s))
+        for n, a, b, s in writes:
+            if n not in bank:
+                wr[n][a:b:s] = [me] * len(range(a, b, s))
+
+    def val(x):
+        return x[0] if isinstance(x, tuple) else x
+
+    def reg(*xs):
+        return [r for x in xs if isinstance(x, tuple) for r in x[1]]
+
+    def cp(o, i):
+        op("v", lambda: g.vector.tensor_copy(o[0], i[0]), i[1], o[1])
+
+    def ts(o, i, s1, o0, s2=None, o1=None):
+        if o1 is None:
+            op("v", lambda: g.vector.tensor_scalar(o[0], i[0], val(s1), None, o0), reg(i, s1), o[1])
+        else:
+            op("v", lambda: g.vector.tensor_scalar(o[0], i[0], val(s1), val(s2), o0, o1), reg(i, s1, s2), o[1])
+
+    def tt(o, a, b, o0):
+        op("v", lambda: g.vector.tensor_tensor(o[0], a[0], b[0], o0), reg(a, b), o[1])
+
+    def scan(o, d0, d1, init, o0, o1):
+        op("v", lambda: g.vector.tensor_tensor_scan(o[0], d0[0], d1[0], init, o0, o1), reg(d0, d1), o[1])
+
+    def fill(o, c):
+        op("v", lambda: g.vector.memset(o[0], c), [], o[1])
+
+    def quant(qc, qs, a, b, src):
+        c, s = V(qc, a, b), V(qs, a, b)
+        op("v", lambda: g.vector.quantize_mx(c[0], s[0], src[0]), src[1], c[1] + s[1])
+
+    def act(o, i, f, bias=0.0, scale=1.0, accum=None):
+        if accum is None:
+            op("a", lambda: g.scalar.activation(o[0], i[0], f, bias=val(bias), scale=val(scale)), reg(i, bias, scale), o[1])
+        else:
+            op("a", lambda: g.scalar.activation(o[0], i[0], f, bias=val(bias), scale=val(scale), accum_out=accum[0]),
+               reg(i, bias, scale), o[1] + accum[1])
+
+    def afill(o, c):
+        n, a, b, s = o[1][0]
+        act(o, V("ONE", 0, len(range(a, b, s))), AF.Identity, scale=float(c))
+
+    def aff(q, o, i, scale, bias):
+        if q == "a":
+            act(o, i, AF.Identity, bias=float(bias), scale=float(scale))
+        else:
+            ts(o, i, float(scale), MUL, float(bias), ADD)
+
+    def move(q, o, i):
+        if q == "a":
+            op("a", lambda: g.scalar.activation(o[0], i[0], AF.Copy), i[1], o[1])
+        else:
+            cp(o, i)
+
+    def mm(b, lq, ls, la, rq, rs, ra, rb, start=True, stop=True):
+        o, l1, l2, r1, r2 = V("ps%d" % b, 0, rb - ra), V(lq, la, la + 128), V(ls, la, la + 128), V(rq, ra, rb), V(rs, ra, rb)
+        op("p", lambda: g.tensor.matmul_mx(o[0], l1[0], l2[0], r1[0], r2[0], start, stop), reg(l1, l2, r1, r2), o[1], acc=not start)
+
+    def iota(o, pat, base, cm=0, small=True):
+        if small:
+            op("g", lambda: g.iota(o[0], pat, base, cm, allow_small_or_imprecise_dtypes=True), [], o[1])
+        else:
+            op("g", lambda: g.iota(o[0], pat, base, cm), [], o[1])
+
+    def sel(o, i, pat, cmpop, base, cm):
+        op("g", lambda: g.affine_select(o[0], i[0], pat, cmpop, 0.0, base, cm), i[1], o[1])
+
+    def dma(q, o, i, reads, writes):
+        op(q, lambda: Q[q].dma_start(o, i), reads, writes, dma=True)
+
+    def bits(v):
+        return v[0].bitcast(dt.uint8)
+
+    xw = V("XS")
+    dma("s", xw[0], T.x[:, :], [], xw[1])
+    dma("a", V("Ub")[0], T.u[:, :], [], V("Ub")[1])
+    for e in range(4):
+        d = V("NBI", 20 * e, 20 * e + 20)
+        dma("s", d[0], T.nb[e:128:4, :], [], d[1])
+    dma("s", bits(V("QW")), T.wc[:, :], [], V("QW")[1])
+    dma("s", V("SW")[0], T.ws[:, :], [], V("SW")[1])
+    dma("s", V("Vb")[0], T.v[:, :], [], V("Vb")[1])
+
+    R_, SC, NSC, ISC, CB_ = col("CF", 0), col("CF", 1), col("CF", 2), col("CF", 3), col("CF", 4)
+    fill(V("ONE"), 1.0)
+    iota(col("PI", 0), [[0, 1]], 0, 1, small=False)
+    iota(V("I16"), [[1, 16]], 0)
+    iota(V("M16"), [[16, 20]], 0)
+    iota(V("O16I"), [[16, 8]], 0, small=False)
+    iota(V("M4"), [[4, 20]], 0)
+    sel(V("BL1"), V("ONE"), [[-16, 8], [0, 64]], AluOpType.is_ge, 0, 1)
+    sel(V("BL2"), V("BL1"), [[16, 8], [0, 64]], AluOpType.is_ge, 15, -1)
+    iota(V("T16B"), [[0, 20], [1, 16]], 0)
+    iota(V("AR", 0, 192), [[1, 192]], 0)
+    iota(V("AR", 192, 320), [[1, 128]], 0)
+    iota(V("AR", 320, 384), [[1, 64]], 0)
+    iota(V("TM1"), [[1, 336]], -1)
+    for k in (1, 2, 3):
+        iota(V("AA", k, 1600, 5), [[0, C]], 0)
+    iota(V("T3", 0, C), [[1, C]], 0)
+    iota(V("T3", C, 2 * C), [[1, C]], U3)
+    iota(V("APS"), [[0, ND], [1, C]], -160)
+    iota(V("LR"), [[0, C]], 0)
+    iota(V("TT", 4 * C), [[0, 256]], 0)
+    for b in range(4):
+        sel(V("EB", 512 * b, 512 * b + 512), V("ONE"), [[-4, 128], [-1, 4]], EQ, b, 4)
+    iota(V("ZS", 0, 256), [[0, 256]], 0)
+    iota(V("T4"), [[4, C]], 0)
+    iota(V("I2K"), [[2048, C]], 0)
+
+    afill(V("CA", 4 * 336), 0.0)
+    afill(V("CA", 4 * 144, 4 * 192), 0.0)
+    afill(V("CA", 4 * 272, 4 * 320), 0.0)
+    ts(col("CI", 0), col("PI", 0), 15, AND)
+    ts(col("CI", 1), col("PI", 0), 3, AND)
+    cp(R_, col("CI", 0))
+    ts(V("W16", 16, 32), V("I16"), 0.0, EQ, -2 * BIG, MUL)
+    ts(V("D16"), V("I16"), R_, SUB)
+    ts(V("ORR"), V("M16"), 0.0, MUL, R_, ADD)
+    ts(V("W16", 48, 64), V("D16"), 0.0, EQ, 0.5, SUB)
+    ts(col("CI", 2), col("CI", 0), 2, SHR)
+    ts(V("W16", 0, 16), V("W16", 48, 64), 2 * BIG, MUL)
+    cp(V("O16"), V("O16I"))
+    move("a", V("LM"), IND(V("W16", 0, 16), V("ORR")))
+    move("a", V("A3"), IND(V("W16", 16, 32), V("ORR")))
+    afill(V("CC", 4 * 272), 0.0)
+    afill(V("CB", 4 * 208), 0.0)
+    afill(V("ONEF"), 1.0)
+    ts(V("W16", 64, 80), V("D16"), 1.0, EQ, P60, MUL)
+    ts(V("W16", 80, 96), V("D16"), 0.0, NE)
+    cp(V("CF", 5, 7), V("CI", 1, 3))
+    ts(SC, R_, 15.0, LT, P60, MUL)
+    ts(col("CF", 7), R_, 15.0, EQ)
+    tt(V("W16", 32, 48), V("W16", 64, 80), V("W16", 80, 96), MAX)
+    ts(CB_, col("CF", 5), 80.0, MUL, col("CF", 6), ADD)
+    ts(SC, SC, 1.0, MAX)
+    ts(ISC, col("CF", 7), 1.0 / P60, MAX)
+
+    quant("QU", "SU", 0, 128, V("Ub"))
+    quant("QX", "SX", 0, C, xw)
+    o16 = V("O16")
+    op("v", lambda: g.vector.tensor_copy(T.QU2[:, 0:128].bitcast(dt.uint32), T.QU[:, 0:128].bitcast(dt.uint32).indirect(o16[0])),
+       reg(V("QU"), o16), V("QU2")[1])
+    cp(V("SU2"), IND(V("SU"), o16))
+    ts(V("NQ"), V("NBI"), 0.0125, MUL, -0.49375, ADD)
+    ts(V("C0"), V("M4"), CB_, ADD)
+    cp(V("NQI"), V("NQ"))
+    ts(NSC, SC, -1.0, MUL)
+
+    def step(G, K, tab, lst, scale, bias):
+        def gat(q, e, a, b):
+            aff(q, V(G, 80 * a + e, 80 * b, 5), IND(tab, V(lst, 20 * e + a, 20 * e + b)), scale, bias)
+
+        def run(a, b):
+            scan(V(K, 80 * a, 80 * b), V("AA", 80 * a, 80 * b), V(G, 80 * a, 80 * b), 0.0, ADD, MIN)
+        for e, q in ((0, "v"), (2, "a"), (1, "v"), (3, "a")):
+            gat(q, e, 0, SPLIT)
+        for e in (1, 2, 3):
+            gat("a", e, SPLIT, 20)
+        run(0, SPLIT)
+        gat("v", 0, SPLIT, 20)
+        run(SPLIT, 20)
+
+    def count_pass(K, between=None):
+        kr = V(K, 4, 1600, 5)
+        for a, b in ((0, 16 * NA), (16 * NA, C)):
+            scan(V("HOR", a, b), V("HH", a, b), V(K, 5 * a + 4, 5 * b, 5), 0.0, MUL, ADD)
+        for m in range(NA):
+            act(V("JK", C * m, C * m + C), kr, AF.Sign, bias=col("HOR", 16 * m + 15), scale=NSC, accum=col("PL", m))
+        for i in range(ND):
+            ts(V("CMP", C * i, C * i + C), kr, SC, MUL, col("HOR", 16 * (NA + i) + 15), LT)
+        if between is not None:
+            between()
+        scan(V("CMS"), V("APS"), V("CMP"), 0.0, MIN, ADD)
+        ts(V("PL", NA, 20), V("CMS", C - 1, C * ND, C), 2.0, MUL, 1.0, ADD)
+
+    def evac(banks, dst, d0, n, p0, relu):
+        for b in range(4):
+            o, i = V(dst, 4 * d0 + b, 4 * (d0 + n), 4), V("ps%d" % banks[b], p0, p0 + n)
+            if b % 2:
+                act(o, i, AF.Relu if relu else AF.Identity, scale=0.03125 if relu else 0.5)
+            elif relu:
+                ts(o, i, 0.0, MAX, 0.03125, MUL)
+            else:
+                ts(o, i, 0.5, MUL)
+
+    def names_of(e):
+        move("a", V("RR", C * e, C * e + C), IND(V("CN"), V("N1", 20 * e, 20 * e + 20)))
+
+    def names_out(q, e):
+        move(q, V("ONB", e, 4 * C, 4), IND(V("RR", C * e, C * e + C), V("OP")))
+
+    for r in range(ROUNDS):
+        last = r == ROUNDS - 1
+        cw, cwn, qt, st = V("CW", 20 * r, 20 * r + 20), V("CW", 20 * r + 20, 20 * r + 40), "QT%d" % r, "STT%d" % r
+        mm(0, "QU2", "SU2", 0, "QX", "SX", 0, C)
+        mm(1, "QU2", "SU2", 0, "QX", "SX", 0, C)
+        for a, b in ((208, C), (0, 208)):
+            tt(V("M3", a, b), V("ps0", a, b), V("LM", a, b), MIN)
+            scan(V("H3", a, b), V("A3", a, b), V("M3", a, b), 0.0, ADD, MAX)
+        own = [19, 18, 17, 16, 15, 14, 13]
+
+        def sign(i):
+            m = own[i]
+            act(V("SG", C * i, C * i + 16 * m), V("ps1", 0, 16 * m), AF.Sign, bias=col("H3", 16 * m + 15), scale=-1.0)
+
+        def relu(i):
+            m = own[i]
+            o = V("CC", m - 16, 64 * m, 4) if m > 16 else V("CB", m - 13, 64 * m, 4)
+            act(o, V("SG", C * i, C * i + 16 * m), AF.Relu, accum=col("RS", m))
+        sign(0)
+        for i in range(7):
+            if i < 6:
+                sign(i + 1)
+            relu(i)
+        tt(V("CC", 0, 4 * C, 4), V("ps0", 0, C), V("H3"), LE)
+        for m in range(12, 0, -1):
+            c, t = (m - 1) // 4, (m - 1) % 4
+            ts(V("CA", 4 * CH[c] + t, 4 * CH[c] + 64 * m, 4), V("ps0", 0, 16 * m), col("H3", 16 * m + 15), LT)
+            if r == 0 and m == 8:
+                ts(V("NQ2"), V("NQI"), -79.75, MUL)
+                ts(V("CNT"), V("M16"), R_, SUB, 16.0, ADD)
+                cp(cw, V("C0"))
+                tt(V("POS"), V("NBI"), V("NQ2"), ADD)
+        if r == 0:
+            quant("QB", "SB", 0, 128, V("BL2"))
+        quant("QCC", "SCC", 0, C, V("CC"))
+        mm(2, "QB", "SB", 0, "QCC", "SCC", 0, C, True, False)
+        wa = 448 if r == 0 else 384
+        quant("QCA", "SCA", 0, wa, V("CA", 0, 4 * wa))
+        for c in range(3):
+            mm(2, "QB", "SB", 0, "QCA", "SCA", CH[c], CH[c] + (192 if c == 2 else 128), False, False)
+        scan(V("RD"), V("T16B"), V("CC", 0, 4 * C, 4), 0.0, MIN, ADD)
+        for t in range(4):
+            if t == 1:
+                quant("QCB", "SCB", 0, 256, V("CB"))
+                mm(2, "QB", "SB", 0, "QCB", "SCB", 0, 256, False, True)
+                move("a", V("CS"), V("ps2", 0, C))
+                tt(V("UT"), V("CNT"), V("RD", 15, C, 16), SUB)
+            if t == 3:
+                tt(V("UT", 13, 20), V("UT", 13, 20), V("RS", 13, 20), SUB)
+            scan(V("RO", t, 4 * 384, 4), V("AR"), V("CA", t, 4 * 384, 4), 0.0, MIN, ADD)
+        for c in range(3):
+            e = 4 * (CH[c] + 64 * c + 63)
+            tt(V("UT", 1 + 4 * c, 5 + 4 * c), V("UT", 1 + 4 * c, 5 + 4 * c), V("RO", e, e + 4), SUB)
+        cp(V("UO"), V("UT"))
+        if r == 0:
+            afill(V("AA", 0, 1600, 5), 1e9)
+            afill(V("AA", 1600, 1616), 1000.0)
+            afill(V("M5"), 1.0)
+        tt(V("BYK"), IND(V("TM1"), V("UO")), V("CS"), ADD)
+        aff("a", V("G2", 4, 1600, 5), IND(V("BYK"), cw), 2.0 ** 20, 0.5)
+        cp(V("AA", 4, 1600, 5), IND(V("BYK"), cw))
+        if r == 0:
+            for e in range(4):
+                act(V("NALL", e, 100, 5), V("POS", 20 * e, 20 * e + 20), AF.Identity, scale=4.0)
+            act(V("NALL", 4, 100, 5), V("M16"), AF.Identity, bias=R_)
+            act(V("M5", 4, 100, 5), V("NALL", 4, 100, 5), AF.Identity, bias=-1596.0, scale=5.0)
+            move("a", V("HH"), IND(V("W16", 32, 48), V("ORR")))
+        scan(V("ST"), V("G2", 4, 1600, 5), V("ONEF"), 1000.0, MIN, ADD)
+        if r == 0:
+            ts(V("N1"), V("POS"), 4.0, MUL)
+        ts(V("EQ"), V("NALL"), col("ST", C - 1), ADD, 320.5, EQ)
+        scan(V("EQS"), V("EQ"), V("M5"), 0.0, MAX, MUL)
+        ts(V("O1"), V("EQS", 4, 100, 5), 1600.0, ADD)
+        cp(V("K1"), IND(V("AA"), V("O1")))
+        step("G2", "K2", V("K1"), "N1", 320.0, 1.0)
+        if not last:
+            aff("a", V("C4"), IND(V("T3", 0, C), cw), 4.0, 0.0)
+
+        def unplaced():
+            if r == 0:
+                ts(V("C2"), V("C0"), 2.0, MUL, 321.0, ADD)
+                ts(V("N5"), V("POS"), 20.0, MUL, 4.0, ADD)
+            ts(V("Y1"), V("HOR", 15, C, 16), ISC, MUL, -200000.0, ADD)
+            tt(V("T2"), V("Y1"), V("C2"), MIN)
+        count_pass("K2", unplaced)
+        tt(V("PM"), V("PL"), V("T2"), MAX)
+        ts(V("O2"), V("PM"), 319.0, ADD, 0.5, MUL)
+        cp(V("CAP"), IND(V("T3"), V("O2")))
+        move("a", V("G3", 4, 1600, 5), IND(V("T3"), V("O2")))
+        step("G3", "K3", V("CAP"), "N1", 320.0, 320.0)
+        aff("a", V("G4", 4, 1600, 5), V("CAP"), 256.0, -SH - 256.0 * 320)
+        step("G4", "K4", V("K3"), "N5", 320.0, 320.0 - SH)
+        count_pass("K4")
+        ts(cwn, V("PL"), -0.5, MUL, 159.5, ADD)
+        lr, c4 = IND(V("LR"), cwn), V("C4L" if last else "C4")
+        op("v", lambda: g.vector.tensor_copy(lr[0], c4[0]), reg(c4, cwn), V("LR")[1])
+        if last:
+            move("a", V("CN"), IND(V("T3", 0, C), cwn))
+            for e in range(3):
+                names_of(e)
+        scan(V("HL"), V("HH"), V("LR"), 0.0, MUL, ADD)
+        order = (1, 0, 3, 2)
+        if last:
+            ts(V("VI"), V("HL", 15, C, 16), ISC, MUL)
+            ts(V("LO"), V("VI"), 2047, AND)
+            for t in order:
+                ts(V("OT", 20 * t, 20 * t + 20), V("LO"), float(t), ADD)
+        else:
+            for t in order:
+                ts(V("OT", 20 * t, 20 * t + 20), V("HL", 15, C, 16), ISC, MUL, float(t), ADD)
+        for t in order:
+            move("a" if t % 2 else "v", V("TT", 1024 + t, 1280, 4), IND(xw, V("OT", 20 * t + 16, 20 * t + 20)))
+        quant(qt, st, 320, 448, V("TT", 1024, 1536))
+        for e in set(wr[qt][320:384]):
+            need("g", e[0], e[1])
+        g.remote_dma(T[qt][:, 0:KB].bitcast(dt.uint8), T[qt][:, 320:384].bitcast(dt.uint8), T.sem["arr%d" % r], T.sem.sent, pid, rid, emask)
+        g.remote_dma(T[st][:, 0:KB], T[st][:, 320:384], T.sem["arr%d" % r], T.sem.sent, pid, rid, emask)
+        for n in (qt, st):
+            wr[n][0:KB] = [("arr%d" % r, 2 * neng)] * KB
+        for t in order:
+            move("a" if t % 2 else "v", V("TT", t, 1024, 4), IND(xw, V("OT", 20 * t, 20 * t + 16)))
+        quant(qt, st, 64, 320, V("TT", 0, 1024))
+        if r == 0:
+            quant("QE", "SE", 0, 512, V("EB"))
+        for b in range(4):
+            mm(b, "QE", "SE", 128 * b, qt, st, 128, 384, True, False)
+            mm(b, "QE", "SE", 128 * b, qt, st, 64, 320, False, True)
+        for b in range(4):
+            mm(4 + b, "QE", "SE", 128 * b, qt, st, 64, 192, True, False)
+        for b in range(4):
+            mm(4 + b, "QE", "SE", 128 * b, qt, st, 0, 128, False, True)
+        if last:
+            ts(V("HI"), V("VI"), 11, SHR)
+            names_of(3)
+            cp(V("OP"), V("HI"))
+            quant("QV", "SV", 0, 128, V("Vb"))
+            names_out("a", 0)
+        else:
+            ts(V("C2"), V("PL"), -1.0, MUL, 640.0, ADD)
+            if r == ROUNDS - 2:
+                tt(V("C4L"), IND(V("T4"), cwn), V("I2K"), ADD)
+        evac((0, 1, 2, 3), "ZS", 128, 256, 0, False)
+        quant("QZ", "SZ", 128, 384, V("ZS", 512, 1536))
+        for b in range(4):
+            mm(b, "QW", "SW", 128 * b, "QZ", "SZ", 128, 384)
+        evac((4, 5, 6, 7), "ZS", 64, 64, 0, False)
+        quant("QZ", "SZ", 0, 128, V("ZS", 0, 512))
+        for b in range(4):
+            mm(4 + b, "QW", "SW", 128 * b, "QZ", "SZ", 0, 128)
+        evac((0, 1, 2, 3), "XS", 64, 256, 0, True)
+        evac((4, 5, 6, 7), "XS", 0, 64, 64, True)
+        quant("QX", "SX", 0, C, xw)
+
+    mm(0, "QV", "SV", 0, "QX", "SX", 0, C)
+    dma("s", T.oc[:, :], bits(V("QX")), V("QX")[1], [])
+    names_out("a", 1)
+    names_out("v", 2)
+    cp(V("YS"), V("ps0", 0, C))
+    for k in range(4):
+        dma("s", T.osc[4 * k:4 * k + 4, :], T.SX[32 * k:32 * k + 4, 0:C], V("SX")[1], [])
+    names_out("a", 3)
+    dma("s", T.y[:, :], V("YS")[0], V("YS")[1], [])
+    dma("a", T.on[:, :], T.ONB[0:128:16, :], V("ONB")[1], [])
+    for sem in sorted(count):
+        need("g", sem, count[sem])
+    g.wait_ge(T.sem.sent, 2 * neng * ROUNDS)

@@ -1,52 +1,83 @@
-from concourse.mybir import dt, AluOpType, ActivationFunctionType
+from concourse.mybir import dt, AluOpType, AxisListType, ActivationFunctionType
 
 C, KB, ROUNDS = 320, 64, 3
-NA = 12
+NA = 13
+NE = 6
+NH = 0
 ND = 20 - NA
-SPLIT = 10
+PIECES = ((128, 320, 0, 0), (0, 128, 4, 2))
+PARTS = ((0, 14, 2), (14, 20, 0))
+PARTS3 = ((0, 12, 2), (12, 20, 0))
+PARTS4 = ((0, 10, 2), (10, 20, 1))
 BIG = 1e28
 P60 = 2.0 ** 60
-SH = 320.0 * 52428
-U3 = 131072
+INF = 2.0 ** 23
+EPS = 2.0 ** -23
+TOP = 75.5
 F32, BF, I32, U16, Q4, U8 = "float32", "bfloat16", "int32", "uint16", "float8_e4m3fn_x4", "uint8"
-CH = (320, 192, 0)
+Q0 = (0, 64, 128, 192, 192)
+STAGES = ((128, 320, 0), (0, 128, 2))
+AHEAD = False
+TAKES = ((128, 320), (0, 128))
+HALVES = ((0, 20),)
+SPLIT = {1: ((0, 20),), 2: ((0, 10), (10, 20))}
+Q_SD, Q_K1, Q_AA, Q_NF, Q_R = "v", "v", "e", "a", "a"
+FREE = "av"
+EVAC = "eeee"
+TAKE = "eeee"
+CALL_V, CALL_A, CALL_P, CALL_D, PE, LEAST = 20.0, 20.0, 20.0, 600.0, 0.5, 64.0
+CYCLE, GATHER, SCATTER, WAKE, LEAN = 0.85, 1.8, 5.0, (120.0, 260.0), (0.0, 0.0, 50.0, 50.0)
+RING = (3000.0, 1800.0, 1800.0)
+RUNS = "aaaavvvv" + "aaaaaavvvvv"
+TILES = (4, 3, 2, 0, 1)
 
 _S = {
-    "XS": (BF, 4 * C), "ZS": (BF, 4 * 384), "TT": (BF, 4 * 384), "QX": (Q4, C), "SX": (U8, C),
-    "QZ": (Q4, 384), "SZ": (U8, 384), "QW": (Q4, 512), "SW": (U8, 512),
+    "XS": (BF, 4 * C), "ZS": (BF, 4 * C), "TT": (BF, 4 * (C + KB)), "QX": (Q4, C), "SX": (U8, C),
+    "QZ": (Q4, C), "SZ": (U8, C), "QW": (Q4, 512), "SW": (U8, 512),
     "Ub": (BF, 512), "QU": (Q4, 128), "SU": (U8, 128), "QU2": (Q4, 128), "SU2": (U8, 128),
     "Vb": (BF, 512), "QV": (Q4, 128), "SV": (U8, 128),
-    "ONE": (BF, 512), "BL1": (BF, 512), "BL2": (BF, 512), "QB": (Q4, 128), "SB": (U8, 128),
-    "EB": (BF, 2048), "QE": (Q4, 512), "SE": (U8, 512),
-    "NBI": (I32, 80), "NQ": (F32, 80), "NQI": (I32, 80), "NQ2": (F32, 80), "POS": (F32, 80),
-    "N1": (U16, 80), "N5": (U16, 80), "NALL": (F32, 100), "M5": (F32, 100), "EQ": (F32, 100), "EQS": (F32, 100),
-    "PI": (I32, 8), "CI": (I32, 8), "CF": (F32, 8), "O16I": (I32, 8), "O16": (U16, 8), "ORR": (U16, 20),
-    "I16": (F32, 16), "D16": (F32, 16), "W16": (F32, 96),
-    "M16": (F32, 20), "M4": (F32, 20), "CNT": (F32, 20), "C0": (F32, 20),
-    "T16B": (BF, C), "HH": (F32, C), "LM": (F32, C), "A3": (F32, C), "ONEF": (F32, C), "AR": (BF, 384), "APS": (BF, C * ND),
-    "TM1": (F32, 336), "T3": (F32, 640), "T4": (F32, C), "I2K": (F32, C),
-    "M3": (F32, C), "H3": (F32, C), "RD": (BF, C), "CA": (BF, 4 * 448), "CB": (BF, 4 * 256), "CC": (BF, 4 * C),
-    "QCA": (Q4, 448), "SCA": (U8, 448), "QCB": (Q4, 256), "SCB": (U8, 256), "QCC": (Q4, C), "SCC": (U8, C),
-    "RO": (BF, 4 * 384), "SG": (BF, 7 * C), "RS": (F32, 20), "UT": (F32, 20), "UO": (U16, 20),
-    "CS": (F32, C), "BYK": (F32, C), "AA": (F32, 1616), "ST": (F32, C), "O1": (U16, 20), "K1": (F32, C),
-    "G2": (F32, 1600), "G3": (F32, 1600), "G4": (F32, 1600), "K2": (F32, 1600), "K3": (F32, 1600), "K4": (F32, 1600),
-    "HOR": (F32, C), "JK": (BF, C * NA), "CMP": (BF, C * ND), "CMS": (BF, C * ND), "PL": (F32, 20),
-    "Y1": (F32, 20), "T2": (F32, 20), "C2": (F32, 20), "PM": (F32, 20), "O2": (U16, 20), "CAP": (F32, C),
-    "CW": (U16, 80),
-    "C4": (F32, C), "C4L": (F32, C), "LR": (F32, C), "HL": (F32, C), "OT": (U16, 80), "VI": (I32, 20), "LO": (I32, 20),
-    "HI": (I32, 20), "OP": (U16, 20), "CN": (F32, C), "RR": (F32, 4 * C), "ONB": (F32, 4 * C), "YS": (F32, C),
+    "ONE": (BF, 516), "BL1": (BF, 512), "BL2": (BF, 512), "QB": (Q4, 128), "SB": (U8, 128),
+    "EB": (BF, 1032), "QE": (Q4, 512), "SE": (U8, 512),
+    "NBI": (I32, 80), "O16I": (I32, 8), "O16": (U16, 8), "ORR": (U16, 20), "W16": (F32, 128),
+    "T16B": (BF, C), "HH": (F32, C), "HHB": (BF, C), "LM": (F32, C), "A3": (F32, C), "Z16": (F32, C),
+    "APS": (BF, C * ND), "T3": (F32, C), "T4K": (F32, C),
+    "M3": (F32, C), "H3": (F32, C), "RD": (BF, C), "CT": (BF, 5 * 4 * C), "QC": (Q4, 5 * C), "SQC": (U8, 5 * C), "ZT": (BF, 4 * 192),
+    "RO": (BF, 20 * C), "SG": (BF, 20 * C), "RM": (F32, C), "NFF": (BF, C), "NFC": (BF, C), "HC": (F32, C),
+    "SF": (BF, 336), "SD": (BF, C), "K1S": (BF, C), "D0S": (BF, C), "BYC": (BF, C), "BYF": (BF, C), "HB": (BF, C),
+    "AA": (F32, 5 * C), "AB": (F32, 7 * C), "K1": (F32, C), "G": (F32, 5 * C), "G4": (F32, 7 * C),
+    "K2": (F32, 5 * C), "K3": (F32, 5 * C), "K4": (F32, 7 * C), "EX": (F32, C), "F3": (F32, C), "E3": (F32, C),
+    "HOR": (F32, C), "JK": (BF, C * NA), "CMP": (BF, C * ND), "CMS": (BF, C * ND),
+    "CMH": (BF, 1280), "CMG": (BF, 1280), "APH": (BF, 1280),
+    "PK": (F32, C), "LR": (F32, C), "HL": (F32, C), "CN": (F32, C), "RR": (F32, 4 * C), "ONB": (F32, 4 * C), "YS": (F32, C),
 }
+_SMALL = {
+    F32: (("NQ", 80), ("NQ2", 80), ("POS", 80), ("NALL", 100), ("M5", 100), ("EQ", 100), ("EQS", 100), ("CF", 16), ("I16", 16),
+          ("D16", 16), ("M16", 20), ("M4", 20), ("CNT", 20), ("C0", 20), ("RS", 20), ("UT", 20), ("US", 20), ("UB", 20), ("PL", 20),
+          ("SC", 16), ("ST", 16), ("FT", 8), ("P0", 20), ("P2", 20)),
+    I32: (("NQI", 80), ("PI", 8), ("CI", 8), ("VI", 20), ("HI", 20)),
+    U16: (("N1", 80), ("N5", 80), ("OS", 2), ("O1", 20), ("BC", 20), ("BF", 20), ("CW", 80), ("OT", 80), ("OP", 20)),
+}
+_AT = {k: (k, 0, v[1]) for k, v in _S.items()}
+for _d, _l in _SMALL.items():
+    _n = 0
+    for _k, _w in _l:
+        _AT[_k] = ("pool_" + _d, _n, _w)
+        _n += (_w + 15) // 16 * 16
+    _S["pool_" + _d] = (_d, _n)
 for _r in range(ROUNDS):
-    _S["QT%d" % _r] = (Q4, 448)
-    _S["STT%d" % _r] = (U8, 448)
+    for _k, _d in (("QT%d" % _r, Q4), ("STT%d" % _r, U8)):
+        _S[_k] = (_d, C + 2 * KB)
+        _AT[_k] = (_k, 0, C + 2 * KB)
 SCRATCH = {k: ("sbuf", [128, v[1]], v[0]) for k, v in _S.items()}
 for _b in range(8):
     SCRATCH["ps%d" % _b] = ("psum", [128, 512], F32)
-NDMA = 16
+    _AT["ps%d" % _b] = ("ps%d" % _b, 0, 512)
+NDMA, LOADS = 32, 10
 SEMAPHORES = ["qv", "qa", "qp", "qg", "sent"] + ["arr%d" % r for r in range(ROUNDS)] + ["d%d" % i for i in range(NDMA)]
 
 ADD, SUB, MUL, MAX, MIN = AluOpType.add, AluOpType.subtract, AluOpType.mult, AluOpType.max, AluOpType.min
-LT, LE, EQ, NE = AluOpType.is_lt, AluOpType.is_le, AluOpType.is_equal, AluOpType.not_equal
+LT, LE, EQ, NEQ = AluOpType.is_lt, AluOpType.is_le, AluOpType.is_equal, AluOpType.not_equal
+GT = AluOpType.is_gt
 AND, SHR = AluOpType.bitwise_and, AluOpType.arith_shift_right
 AF = ActivationFunctionType
 
@@ -63,14 +94,14 @@ def rank_program(g, core, T, topo):
     Q = {"v": g.vector, "a": g.scalar, "p": g.tensor, "g": g, "s": g.sync}
     count, known, clock = {}, {q: {} for q in Q}, {}
     wr = {k: [None] * v[1] for k, v in _S.items()}
-    rd = {k: {} for k in _S}
-    bank = {"ps%d" % b: {} for b in range(8)}
-    ndma = [0]
+    rd = {k: [] for k in _S}
+    bank = {"ps%d" % b: [None, [], []] for b in range(8)}
+    ndma, ops = [0], []
 
     def V(name, a=0, b=None, s=1):
-        if b is None:
-            b = 512 if name in bank else _S[name][1]
-        return (T[name][:, a:b] if s == 1 else T[name][:, a:b:s], [(name, a, b, s)])
+        buf, at, n = _AT[name]
+        a, b = at + a, at + (n if b is None else b)
+        return (T[buf][:, a:b] if s == 1 else T[buf][:, a:b:s], [(buf, a, b, s)])
 
     def col(name, j):
         return V(name, j, j + 1)
@@ -87,49 +118,89 @@ def rank_program(g, core, T, topo):
                 known[q][s2] = v2
         known[q][sem] = val
 
-    def op(q, call, reads, writes, dma=False, acc=False):
-        deps = {}
-
-        def dep(e):
-            if e is not None and deps.get(e[0], 0) < e[1]:
-                deps[e[0]] = e[1]
+    def op(q, call, reads, writes, cost, after=0.0, event=None, acc=False):
+        me, deps, behind = len(ops), set(), set()
+        for n in set(r[0] for r in reads + writes if r[0] in bank):
+            k = bank[n]
+            if k[0] != q or q == "e":
+                k[0], k[1], k[2] = q, [], k[1]
+            deps.update(k[2])
+            if q == "p":
+                (behind if acc else deps).update(k[1][-1:])
+            k[1].append(me)
         for n, a, b, s in reads + writes:
-            if n in bank:
-                for q2, e in bank[n].items():
-                    if q2 != q or (q == "p" and not acc):
-                        dep(e)
-        for n, a, b, s in reads:
             if n not in bank:
-                for e in set(wr[n][a:b:s]):
-                    dep(e)
+                deps.update(wr[n][a:b:s])
         for n, a, b, s in writes:
             if n not in bank:
-                for e in set(wr[n][a:b:s]):
-                    dep(e)
-                for lst in rd[n].values():
-                    for e in set(lst[a:b:s]):
-                        dep(e)
-        for sem in sorted(deps, key=lambda x: (-len(clock.get((x, deps[x]), {})), x)):
-            need(q, sem, deps[sem])
-        if dma:
-            sem, inc = "d%d" % ndma[0], 16
-            ndma[0] += 1
-        else:
-            sem, inc = "q" + q, 1
-        call().then_inc(T.sem[sem], inc)
-        count[sem] = count.get(sem, 0) + inc
-        me = (sem, count[sem])
-        clock[me] = dict(known[q])
-        for n, a, b, s in reads + writes:
-            if n in bank:
-                bank[n][q] = me
+                mine, keep = set(range(a, b, s)), []
+                for o2, a2, b2, cells in rd[n]:
+                    if a2 < b and a < b2 and not mine.isdisjoint(cells):
+                        deps.add(o2)
+                        if cells <= mine:
+                            continue
+                    keep.append((o2, a2, b2, cells))
+                rd[n] = keep
         for n, a, b, s in reads:
             if n not in bank:
-                lst = rd[n].setdefault(sem, [None] * _S[n][1])
-                lst[a:b:s] = [me] * len(range(a, b, s))
+                rd[n].append((me, a, b, set(range(a, b, s))))
         for n, a, b, s in writes:
             if n not in bank:
                 wr[n][a:b:s] = [me] * len(range(a, b, s))
+        if event == "dma" and len(ops) < LOADS:
+            behind.update(i for i, o in enumerate(ops) if o[0] == q)
+        deps.discard(None)
+        deps.discard(me)
+        ops.append((q, call if q == "e" else {q: call}, deps, behind, cost if q == "e" else {q: cost}, after, event))
+
+    def issue():
+        n = len(ops)
+        before, behind, done = [[] for _ in ops], [[] for _ in ops], [None] * n
+        for i, o in enumerate(ops):
+            for d in o[2] | o[3]:
+                lag = (ops[d][5], True) if d in o[2] else (0.0, False)
+                before[i].append((d,) + lag)
+                behind[d].append((i,) + lag)
+
+        def place(order, links, tail, lean):
+            ends, busy, at = [0.0] * n, {q: [] for q in Q}, [None] * n
+            for i in order:
+                best = None
+                for q, cost in ops[i][4].items():
+                    t, line, k = max([ends[d] + lag + (WAKE[at[d][1] != q] if wait else 0.0) for d, lag, wait in links[i]]
+                                     + [ops[i][5] if tail else 0.0]), busy[q], 0
+                    while k < len(line) and line[k][0] < t + cost:
+                        t = max(t, line[k][1])
+                        k += 1
+                    if best is None or t + cost + lean < best[0]:
+                        best = (t + cost, t, q, k)
+                busy[best[2]].insert(best[3], (best[1], best[0]))
+                ends[i], at[i] = best[0], best[1:3]
+            return ends, at
+        ends, at = kept = place(range(n), before, False, LEAN[0])
+        for lean in LEAN:
+            back = place(sorted(range(n), key=lambda i: (-ends[i] - ops[i][5], -i)), behind, True, lean)[0]
+            ends, at = place(sorted(range(n), key=lambda i: (-back[i], i)), before, False, lean)
+            if max(e + o[5] for e, o in zip(ends, ops)) < max(e + o[5] for e, o in zip(kept[0], ops)):
+                kept = ends, at
+        for k in sorted(range(n), key=lambda i: (kept[1][i][0], i)):
+            q = kept[1][k][1]
+            deps = {}
+            for d in ops[k][2]:
+                deps[done[d][0]] = max(deps.get(done[d][0], 0), done[d][1])
+            for sem in sorted(deps, key=lambda x: (-len(clock.get((x, deps[x]), {})), x)):
+                need(q, sem, deps[sem])
+            event = ops[k][6]
+            if event is None or event == "dma":
+                sem, inc = ("q" + q, 1) if event is None else ("d%d" % ndma[0], 16)
+                ndma[0] += event == "dma"
+                ops[k][1][q]().then_inc(T.sem[sem], inc)
+                count[sem] = count.get(sem, 0) + inc
+                done[k] = (sem, count[sem])
+                clock[done[k]] = dict(known[q])
+            else:
+                ops[k][1][q]()
+                done[k] = event
 
     def val(x):
         return x[0] if isinstance(x, tuple) else x
@@ -137,127 +208,169 @@ def rank_program(g, core, T, topo):
     def reg(*xs):
         return [r for x in xs if isinstance(x, tuple) for r in x[1]]
 
+    def size(v):
+        n, a, b, s = v[1][0]
+        return len(range(a, b, s))
+
+    def cycles(o, i, *more, rate=1.0):
+        if len(i[1]) > 1:
+            return 60.0 + CYCLE * GATHER * size(o)
+        if i[1][0][0] in bank:
+            return CALL_P + CYCLE * max(LEAST, size(o))
+        if rate is None:
+            return CALL_A + CYCLE * max(LEAST, size(o))
+        if all(x[1][0][0] in _S and _S[x[1][0][0]][0] in (BF, U16) for x in (o, i) + more):
+            rate *= 0.5
+        return CALL_V + CYCLE * max(LEAST, rate * size(o))
+
     def cp(o, i):
-        op("v", lambda: g.vector.tensor_copy(o[0], i[0]), i[1], o[1])
+        op("v", lambda: g.vector.tensor_copy(o[0], i[0]), i[1], o[1], cycles(o, i))
 
     def ts(o, i, s1, o0, s2=None, o1=None):
         if o1 is None:
-            op("v", lambda: g.vector.tensor_scalar(o[0], i[0], val(s1), None, o0), reg(i, s1), o[1])
+            op("v", lambda: g.vector.tensor_scalar(o[0], i[0], val(s1), None, o0), reg(i, s1), o[1], cycles(o, i))
         else:
-            op("v", lambda: g.vector.tensor_scalar(o[0], i[0], val(s1), val(s2), o0, o1), reg(i, s1, s2), o[1])
+            op("v", lambda: g.vector.tensor_scalar(o[0], i[0], val(s1), val(s2), o0, o1), reg(i, s1, s2), o[1], cycles(o, i))
 
     def tt(o, a, b, o0):
-        op("v", lambda: g.vector.tensor_tensor(o[0], a[0], b[0], o0), reg(a, b), o[1])
+        op("v", lambda: g.vector.tensor_tensor(o[0], a[0], b[0], o0), reg(a, b), o[1], cycles(o, a, b, rate=1.0 if a[1][0][0] in bank else 2.0))
 
-    def scan(o, d0, d1, init, o0, o1):
-        op("v", lambda: g.vector.tensor_tensor_scan(o[0], d0[0], d1[0], init, o0, o1), reg(d0, d1), o[1])
+    def scan(o, d0, d1, init, o0, o1, start=None):
+        op("v", lambda: g.vector.tensor_tensor_scan(o[0], d0[0], d1[0], init, o0, o1), reg(d0, d1, start), o[1], cycles(o, d0, d1))
+
+    def scatter(win, off, src):
+        o = IND(win, off)
+        op("v", lambda: g.vector.tensor_copy(o[0], src[0]), reg(src, off), win[1], 50.0 + CYCLE * SCATTER * size(src))
 
     def fill(o, c):
-        op("v", lambda: g.vector.memset(o[0], c), [], o[1])
+        op("v", lambda: g.vector.memset(o[0], c), [], o[1], cycles(o, o))
 
     def quant(qc, qs, a, b, src):
         c, s = V(qc, a, b), V(qs, a, b)
-        op("v", lambda: g.vector.quantize_mx(c[0], s[0], src[0]), src[1], c[1] + s[1])
+        op("v", lambda: g.vector.quantize_mx(c[0], s[0], src[0]), src[1], c[1] + s[1], 30.0 + 0.225 * size(src))
 
-    def act(o, i, f, bias=0.0, scale=1.0, accum=None):
+    def act(o, i, f, bias=0.0, scale=1.0, accum=None, more=0.0):
         if accum is None:
-            op("a", lambda: g.scalar.activation(o[0], i[0], f, bias=val(bias), scale=val(scale)), reg(i, bias, scale), o[1])
+            op("a", lambda: g.scalar.activation(o[0], i[0], f, bias=val(bias), scale=val(scale)), reg(i, bias, scale), o[1],
+               cycles(o, i, rate=None) + more)
         else:
             op("a", lambda: g.scalar.activation(o[0], i[0], f, bias=val(bias), scale=val(scale), accum_out=accum[0]),
-               reg(i, bias, scale), o[1] + accum[1])
+               reg(i, bias, scale), o[1] + accum[1], cycles(o, i, rate=None) + 20.0)
 
     def afill(o, c):
         n, a, b, s = o[1][0]
         act(o, V("ONE", 0, len(range(a, b, s))), AF.Identity, scale=float(c))
 
+    def either(o, i, on_a, on_v, reads):
+        op("e", {"a": on_a, "v": on_v}, reads, o[1], {"a": cycles(o, i, rate=None) + 15.0 * (len(i[1]) > 1), "v": cycles(o, i)})
+
     def aff(q, o, i, scale, bias):
         if q == "a":
-            act(o, i, AF.Identity, bias=float(bias), scale=float(scale))
+            act(o, i, AF.Identity, bias=bias, scale=scale)
+        elif q == "v":
+            ts(o, i, scale, MUL, bias, ADD)
         else:
-            ts(o, i, float(scale), MUL, float(bias), ADD)
+            either(o, i, lambda: g.scalar.activation(o[0], i[0], AF.Identity, bias=val(bias), scale=val(scale)),
+                   lambda: g.vector.tensor_scalar(o[0], i[0], val(scale), val(bias), MUL, ADD), reg(i, scale, bias))
 
     def move(q, o, i):
         if q == "a":
-            op("a", lambda: g.scalar.activation(o[0], i[0], AF.Copy), i[1], o[1])
-        else:
+            op("a", lambda: g.scalar.activation(o[0], i[0], AF.Copy), i[1], o[1], cycles(o, i, rate=None))
+        elif q == "v":
             cp(o, i)
+        else:
+            either(o, i, lambda: g.scalar.activation(o[0], i[0], AF.Copy), lambda: g.vector.tensor_copy(o[0], i[0]), i[1])
 
     def mm(b, lq, ls, la, rq, rs, ra, rb, start=True, stop=True):
         o, l1, l2, r1, r2 = V("ps%d" % b, 0, rb - ra), V(lq, la, la + 128), V(ls, la, la + 128), V(rq, ra, rb), V(rs, ra, rb)
-        op("p", lambda: g.tensor.matmul_mx(o[0], l1[0], l2[0], r1[0], r2[0], start, stop), reg(l1, l2, r1, r2), o[1], acc=not start)
+        op("p", lambda: g.tensor.matmul_mx(o[0], l1[0], l2[0], r1[0], r2[0], start, stop), reg(l1, l2, r1, r2), o[1],
+           20.0 + PE * (rb - ra + 16), after=60.0, acc=not start)
 
     def iota(o, pat, base, cm=0, small=True):
         if small:
-            op("g", lambda: g.iota(o[0], pat, base, cm, allow_small_or_imprecise_dtypes=True), [], o[1])
+            op("g", lambda: g.iota(o[0], pat, base, cm, allow_small_or_imprecise_dtypes=True), [], o[1], 160.0 + 3.5 * CYCLE * size(o))
         else:
-            op("g", lambda: g.iota(o[0], pat, base, cm), [], o[1])
+            op("g", lambda: g.iota(o[0], pat, base, cm), [], o[1], 160.0 + 3.5 * CYCLE * size(o))
 
     def sel(o, i, pat, cmpop, base, cm):
-        op("g", lambda: g.affine_select(o[0], i[0], pat, cmpop, 0.0, base, cm), i[1], o[1])
+        op("g", lambda: g.affine_select(o[0], i[0], pat, cmpop, 0.0, base, cm), i[1], o[1], 210.0 + 3.5 * CYCLE * size(o))
 
-    def dma(q, o, i, reads, writes):
-        op(q, lambda: Q[q].dma_start(o, i), reads, writes, dma=True)
+    def dma(q, o, i, reads, writes, lands=2000.0):
+        op(q, lambda: Q[q].dma_start(o, i), reads, writes, CALL_D, after=lands, event="dma")
+
+    def send(r):
+        qt, st, arr = "QT%d" % r, "STT%d" % r, T.sem["arr%d" % r]
+
+        def calls():
+            g.remote_dma(T[qt][:, 0:KB].bitcast(dt.uint8), T[qt][:, C:C + KB].bitcast(dt.uint8), arr, T.sem.sent, pid, rid, emask)
+            g.remote_dma(T[st][:, 0:KB], T[st][:, C:C + KB], arr, T.sem.sent, pid, rid, emask)
+        op("g", calls, reg(V(qt, C, C + KB), V(st, C, C + KB)), reg(V(qt, 0, KB), V(st, 0, KB)), 600.0, after=RING[r], event=("arr%d" % r, 2 * neng))
 
     def bits(v):
         return v[0].bitcast(dt.uint8)
 
     xw = V("XS")
-    dma("s", xw[0], T.x[:, :], [], xw[1])
     dma("a", V("Ub")[0], T.u[:, :], [], V("Ub")[1])
+    for k, (a, b) in enumerate(TAKES):
+        dma("s", V("XS", 4 * a, 4 * b)[0], T.x[:, 4 * a:4 * b], [], V("XS", 4 * a, 4 * b)[1], 2700.0 + 1000.0 * k)
     for e in range(4):
         d = V("NBI", 20 * e, 20 * e + 20)
-        dma("s", d[0], T.nb[e:128:4, :], [], d[1])
-    dma("s", bits(V("QW")), T.wc[:, :], [], V("QW")[1])
-    dma("s", V("SW")[0], T.ws[:, :], [], V("SW")[1])
-    dma("s", V("Vb")[0], T.v[:, :], [], V("Vb")[1])
+        dma("s", d[0], T.nb[e:128:4, :], [], d[1], 4000.0)
+    for o, i, d in ((bits(V("QW")), T.wc, V("QW")), (V("SW")[0], T.ws, V("SW")), (V("Vb")[0], T.v, V("Vb"))):
+        dma("s", o, i[:, :], xw[1], d[1])
 
-    R_, SC, NSC, ISC, CB_ = col("CF", 0), col("CF", 1), col("CF", 2), col("CF", 3), col("CF", 4)
+    R_, SC, ISC, CB_, ISC4, ISCK, R4, CAPB = (col("CF", j) for j in (0, 1, 3, 4, 8, 9, 10, 11))
+    CST, CUP, RR_, S3, B3, T1, T2, NEGA, TOPS, CAD = (col("SC", j) for j in range(10))
     fill(V("ONE"), 1.0)
     iota(col("PI", 0), [[0, 1]], 0, 1, small=False)
     iota(V("I16"), [[1, 16]], 0)
     iota(V("M16"), [[16, 20]], 0)
     iota(V("O16I"), [[16, 8]], 0, small=False)
     iota(V("M4"), [[4, 20]], 0)
-    sel(V("BL1"), V("ONE"), [[-16, 8], [0, 64]], AluOpType.is_ge, 0, 1)
+    iota(V("P0"), [[1, 4], [64, 5]], 0)
+    fill(V("AA", 0, 400), 0.0)
+    sel(V("BL1"), V("ONE", 0, 512), [[-16, 8], [0, 64]], AluOpType.is_ge, 0, 1)
     sel(V("BL2"), V("BL1"), [[16, 8], [0, 64]], AluOpType.is_ge, 15, -1)
+    iota(V("LR"), [[1, 4], [4, 80]], 0)
     iota(V("T16B"), [[0, 20], [1, 16]], 0)
-    iota(V("AR", 0, 192), [[1, 192]], 0)
-    iota(V("AR", 192, 320), [[1, 128]], 0)
-    iota(V("AR", 320, 384), [[1, 64]], 0)
-    iota(V("TM1"), [[1, 336]], -1)
-    for k in (1, 2, 3):
-        iota(V("AA", k, 1600, 5), [[0, C]], 0)
-    iota(V("T3", 0, C), [[1, C]], 0)
-    iota(V("T3", C, 2 * C), [[1, C]], U3)
-    iota(V("APS"), [[0, ND], [1, C]], -160)
-    iota(V("LR"), [[0, C]], 0)
-    iota(V("TT", 4 * C), [[0, 256]], 0)
+    iota(V("T3"), [[1, C]], 0)
+    iota(V("AB", 0, 560), [[0, 560]], 1)
+    iota(V("AB", 0, 560, 7), [[0, 80]], 0)
+    iota(V("APS", 0, C), [[1, C]], -160)
+    iota(V("G4", 6, 7 * C, 7), [[0, C]], 0)
+    sel(V("Z16"), V("ONE", 0, C), [[0, 20], [1, 16]], NEQ, 0, 0)
+    for b in (2, 3):
+        sel(V("EB", 516 * (b - 2), 516 * (b - 1)), V("ONE"), [[-1, 516]], EQ, b, 4)
+    for q in range(4):
+        iota(V("PK", q, C, 4), [[4100, 80]], 327681 * q)
+    iota(V("T4K"), [[4096, C]], 0)
     for b in range(4):
-        sel(V("EB", 512 * b, 512 * b + 512), V("ONE"), [[-4, 128], [-1, 4]], EQ, b, 4)
-    iota(V("ZS", 0, 256), [[0, 256]], 0)
-    iota(V("T4"), [[4, C]], 0)
-    iota(V("I2K"), [[2048, C]], 0)
+        a = 516 * (b % 2) + 2 * (b < 2)
+        quant("QE", "SE", 128 * b, 128 * b + 128, V("EB", a, a + 512))
 
-    afill(V("CA", 4 * 336), 0.0)
-    afill(V("CA", 4 * 144, 4 * 192), 0.0)
-    afill(V("CA", 4 * 272, 4 * 320), 0.0)
+    def repeat(name, w):
+        for a in range(w, _AT[name][2], w):
+            dma("s", V(name, a, a + w)[0], V(name, 0, w)[0], V(name, 0, w)[1], V(name, a, a + w)[1], 3000.0)
+    act(V("AA", 0, 400, 5), V("ONE", 0, 80), AF.Exp, scale=28.0, more=1300.0)
+    repeat("AA", 400)
+    repeat("APS", C)
     ts(col("CI", 0), col("PI", 0), 15, AND)
     ts(col("CI", 1), col("PI", 0), 3, AND)
     cp(R_, col("CI", 0))
-    ts(V("W16", 16, 32), V("I16"), 0.0, EQ, -2 * BIG, MUL)
+    ts(V("W16", 16, 32), V("I16"), 0.0, EQ, 2 * BIG, MUL)
     ts(V("D16"), V("I16"), R_, SUB)
     ts(V("ORR"), V("M16"), 0.0, MUL, R_, ADD)
     ts(V("W16", 48, 64), V("D16"), 0.0, EQ, 0.5, SUB)
     ts(col("CI", 2), col("CI", 0), 2, SHR)
-    ts(V("W16", 0, 16), V("W16", 48, 64), 2 * BIG, MUL)
+    ts(V("W16", 0, 16), V("W16", 48, 64), -2 * BIG, MUL)
     cp(V("O16"), V("O16I"))
     move("a", V("LM"), IND(V("W16", 0, 16), V("ORR")))
     move("a", V("A3"), IND(V("W16", 16, 32), V("ORR")))
-    afill(V("CC", 4 * 272), 0.0)
-    afill(V("CB", 4 * 208), 0.0)
-    afill(V("ONEF"), 1.0)
     ts(V("W16", 64, 80), V("D16"), 1.0, EQ, P60, MUL)
-    ts(V("W16", 80, 96), V("D16"), 0.0, NE)
+    ts(V("W16", 80, 96), V("D16"), 0.0, NEQ)
+    ts(V("W16", 96, 112), V("D16"), 0.0, EQ)
+    move("e", V("AB", 6, 560, 7), IND(V("W16", 96, 112), V("ORR", 0, 5)))
+    repeat("AB", 560)
     cp(V("CF", 5, 7), V("CI", 1, 3))
     ts(SC, R_, 15.0, LT, P60, MUL)
     ts(col("CF", 7), R_, 15.0, EQ)
@@ -265,54 +378,103 @@ def rank_program(g, core, T, topo):
     ts(CB_, col("CF", 5), 80.0, MUL, col("CF", 6), ADD)
     ts(SC, SC, 1.0, MAX)
     ts(ISC, col("CF", 7), 1.0 / P60, MAX)
+    ts(R4, R_, 4.0, MUL)
+    ts(V("FT", 0, 2), V("I16", 0, 2), INF, MUL)
+    ts(CAPB, col("I16", 1), INF - 1024.0, MUL, 2.0 ** 89, MUL)
+    fill(V("M5"), 1.0)
+    fill(V("SF"), 0.0)
+    ts(ISC4, ISC, 2.0 ** -10, MUL)
+    ts(V("OP"), V("P0"), R4, ADD)
+    fill(V("M5", 4, 100, 5), -1.0)
+    ts(V("NALL", 4, 100, 5), V("M16"), R_, ADD)
+    ts(V("C0"), V("M4"), CB_, ADD)
+    ts(V("CNT"), V("M16"), R_, ADD, -160.0, ADD)
+    cp(V("CW", 0, 20), V("C0"))
+    fill(V("RS"), 0.0)
+    cp(V("RO", 20 * C - 20, 20 * C), V("CNT"))
+    fill(V("ZT"), 0.0)
 
     quant("QU", "SU", 0, 128, V("Ub"))
-    quant("QX", "SX", 0, C, xw)
     o16 = V("O16")
     op("v", lambda: g.vector.tensor_copy(T.QU2[:, 0:128].bitcast(dt.uint32), T.QU[:, 0:128].bitcast(dt.uint32).indirect(o16[0])),
-       reg(V("QU"), o16), V("QU2")[1])
+       reg(V("QU"), o16), V("QU2")[1], cycles(V("QU2"), IND(V("QU"), o16)))
     cp(V("SU2"), IND(V("SU"), o16))
+    for k in (4, 3, 2, 1, 0):
+        afill(V("CT", 4 * (C * k + Q0[k]), 4 * (C * k + min(64 * k + 48, C - 16))), 0.0)
+    move("a", V("HH"), IND(V("W16", 32, 48), V("ORR")))
+    for k in (4, 3):
+        quant("QC", "SQC", C * k, C * k + 192, V("ZT"))
+    for a, b in TAKES:
+        quant("QX", "SX", a, b, V("XS", 4 * a, 4 * b))
+    for k in (2, 1):
+        quant("QC", "SQC", C * k, C * k + 128, V("ZT", 0, 512))
     ts(V("NQ"), V("NBI"), 0.0125, MUL, -0.49375, ADD)
-    ts(V("C0"), V("M4"), CB_, ADD)
     cp(V("NQI"), V("NQ"))
-    ts(NSC, SC, -1.0, MUL)
+    ts(V("NQ2"), V("NQI"), -79.75, MUL)
+    tt(V("POS"), V("NBI"), V("NQ2"), ADD)
 
-    def step(G, K, tab, lst, scale, bias):
+    def step(parts, A, G, K, w, tab, lst, scale, o0, o1, before=None, after=None):
         def gat(q, e, a, b):
-            aff(q, V(G, 80 * a + e, 80 * b, 5), IND(tab, V(lst, 20 * e + a, 20 * e + b)), scale, bias)
-
-        def run(a, b):
-            scan(V(K, 80 * a, 80 * b), V("AA", 80 * a, 80 * b), V(G, 80 * a, 80 * b), 0.0, ADD, MIN)
-        for e, q in ((0, "v"), (2, "a"), (1, "v"), (3, "a")):
-            gat(q, e, 0, SPLIT)
-        for e in (1, 2, 3):
-            gat("a", e, SPLIT, 20)
-        run(0, SPLIT)
-        gat("v", 0, SPLIT, 20)
-        run(SPLIT, 20)
-
-    def count_pass(K, between=None):
-        kr = V(K, 4, 1600, 5)
-        for a, b in ((0, 16 * NA), (16 * NA, C)):
-            scan(V("HOR", a, b), V("HH", a, b), V(K, 5 * a + 4, 5 * b, 5), 0.0, MUL, ADD)
-        for m in range(NA):
-            act(V("JK", C * m, C * m + C), kr, AF.Sign, bias=col("HOR", 16 * m + 15), scale=NSC, accum=col("PL", m))
-        for i in range(ND):
-            ts(V("CMP", C * i, C * i + C), kr, SC, MUL, col("HOR", 16 * (NA + i) + 15), LT)
-        if between is not None:
-            between()
-        scan(V("CMS"), V("APS"), V("CMP"), 0.0, MIN, ADD)
-        ts(V("PL", NA, 20), V("CMS", C - 1, C * ND, C), 2.0, MUL, 1.0, ADD)
-
-    def evac(banks, dst, d0, n, p0, relu):
-        for b in range(4):
-            o, i = V(dst, 4 * d0 + b, 4 * (d0 + n), 4), V("ps%d" % banks[b], p0, p0 + n)
-            if b % 2:
-                act(o, i, AF.Relu if relu else AF.Identity, scale=0.03125 if relu else 0.5)
-            elif relu:
-                ts(o, i, 0.0, MAX, 0.03125, MUL)
+            o, i = V(G, 16 * w * a + e, 16 * w * b, w), IND(tab, V(lst, 20 * e + a, 20 * e + b))
+            if scale is None:
+                move(q, o, i)
             else:
-                ts(o, i, 0.5, MUL)
+                aff(q, o, i, scale, 0.0)
+        for a, b, nv in parts:
+            for e in range(nv, 4):
+                gat(FREE[0], e, a, b)
+            if before is not None:
+                before(a, b)
+        for a, b, nv in parts:
+            for e in range(nv):
+                gat(FREE[1], e, a, b)
+            scan(V(K, 16 * w * a, 16 * w * b), V(A, 16 * w * a, 16 * w * b), V(G, 16 * w * a, 16 * w * b), 0.0, o0, o1)
+            if after is not None:
+                after(a, b)
+
+    def own_keys(a, b):
+        scan(V("HOR", a, b), V("Z16", a, b), V("K4", 7 * a + 6, 7 * b, 7), 0.0, MUL, MAX)
+
+    def signs(m, a, b, acc):
+        act(V("JK", C * m + a, C * m + b), V("K4", 7 * a + 5, 7 * b, 7), AF.Sign, bias=col("HOR", 16 * m + 15), scale=-1.0, accum=col(acc, m))
+
+    def count_early(a, b):
+        if a == 0:
+            own_keys(0, 16 * b)
+            for m in range(NE):
+                signs(m, 0, 16 * b, "P2")
+
+    def count_pass(at):
+        kr, h = V("K4", 5, 7 * C, 7), 16 * PARTS4[0][1]
+        own_keys(h, C)
+        for m in range(NH, NA):
+            signs(m, h if m < NE else 0, C, "PL")
+        if NH:
+            n = C - h
+            for m in range(NH):
+                ts(V("CMH", n * m, n * m + n), V("K4", 7 * h + 5, 7 * C, 7), col("HOR", 16 * m + 15), LT)
+            scan(V("CMG", 0, n * NH), V("APH", 0, n * NH), V("CMH", 0, n * NH), 0.0, MIN, ADD)
+            ts(V("PL", 0, NH), V("CMG", n - 1, n * NH, n), 2.0, MUL, -float(n), ADD)
+        for i in range(ND):
+            ts(V("CMP", C * i, C * i + C), kr, col("HOR", 16 * (NA + i) + 15), LT)
+        scan(V("CMS"), V("APS"), V("CMP"), 0.0, MIN, ADD)
+        tt(V("PL", 0, NE), V("PL", 0, NE), V("P2", 0, NE), ADD)
+        ts(V("CW", at + NA, at + 20), V("CMS", C - 1, C * ND, C), 160.0, ADD)
+        ts(V("CW", at, at + NA), V("PL", 0, NA), 0.5, MUL, 159.5, ADD)
+
+    def evac(b, pb, dst, d0, n, relu):
+        o, i = V(dst, 4 * d0 + b, 4 * (d0 + n), 4), V("ps%d" % pb, 0, n)
+        if EVAC[b] == "e" and relu:
+            either(o, i, lambda: g.scalar.activation(o[0], i[0], AF.Relu, scale=0.03125),
+                   lambda: g.vector.tensor_scalar(o[0], i[0], 0.0, 0.03125, MAX, MUL), i[1])
+        elif EVAC[b] == "e":
+            aff("e", o, i, 0.5, 0.0)
+        elif EVAC[b] == "a":
+            act(o, i, AF.Relu if relu else AF.Identity, scale=0.03125 if relu else 0.5)
+        elif relu:
+            ts(o, i, 0.0, MAX, 0.03125, MUL)
+        else:
+            ts(o, i, 0.5, MUL)
 
     def names_of(e):
         move("a", V("RR", C * e, C * e + C), IND(V("CN"), V("N1", 20 * e, 20 * e + 20)))
@@ -320,169 +482,174 @@ def rank_program(g, core, T, topo):
     def names_out(q, e):
         move(q, V("ONB", e, 4 * C, 4), IND(V("RR", C * e, C * e + C), V("OP")))
 
+    def unplaced(cw):
+        aff("a", V("G4", 5, 7 * C, 7), IND(V("T3"), cw), -2.0 ** -111, 832.0 * 2.0 ** -111)
+
+    def pack(cw):
+        for a, b in ((0, 10), (10, 20)):
+            tt(V("PK", 16 * a, 16 * b), IND(V("T4K"), V("CW", cw + a, cw + b)), V("T3", 16 * a, 16 * b), ADD)
+
+    def slot(i, a, b=C):
+        return V("CT", 4 * (C * (i // 4) + a) + i % 4, 4 * (C * (i // 4) + b), 4)
+
+    def compare(lo, hi, pb):
+        pv, pa = "ps%d" % pb, "ps%d" % (pb + 1)
+        narrow = lo == 0 and AHEAD and hi <= 128 and "v" not in RUNS[:hi // 16 - 1]
+        mm(pb, "QU2", "SU2", 0, "QX", "SX", lo, 128 if narrow else C)
+        mm(pb + 1, "QU2", "SU2", 0, "QX", "SX", lo, C)
+        tt(V("M3", lo, hi), V(pv, 0, hi - lo), V("LM", lo, hi), MAX)
+        scan(V("H3", lo, hi), V("A3", lo, hi), V("M3", lo, hi), 0.0, ADD, MIN)
+        if lo == 0 and not AHEAD:
+            scan(V("RM"), V(pv, 0, C), V("ONE", 0, C), -BIG, MAX, MUL)
+            act(V("JK", 0, C), V("RM"), AF.Sign, bias=col("RM", C - 1), scale=-1.0, accum=CST)
+            cp(col("OS", 0), CST)
+        if lo == STAGES[-1][1] and AHEAD:
+            scan(V("RM", lo, C), V(pv, 0, C - lo), V("ONE", lo, C), -BIG, MAX, MUL)
+            act(V("JK", lo, C), V("RM", lo, C), AF.Sign, bias=col("RM", C - 1), scale=-1.0, accum=CUP)
+        if lo == 0 and AHEAD:
+            scan(V("RM", 0, hi), V(pv, 0, hi), V("ONE", 0, hi), -BIG, MAX, MUL)
+            ts(TOPS, col("RM", hi - 1), col("RM", C - 1), MAX)
+            act(V("JK", 0, hi), V("RM", 0, hi), AF.Sign, bias=TOPS, scale=-1.0, accum=CST)
+            ts(CAD, CST, float(hi), EQ, CUP, MUL)
+            ts(col("OS", 0), CST, CAD, ADD)
+        tt(slot(0, lo, hi), V(pv, 0, hi - lo), V("H3", lo, hi), GT)
+        for m in range(lo // 16, min(hi // 16, 19)):
+            a, own = 16 * m + 16, col("H3", 16 * m + 15)
+            if RUNS[m] == "a":
+                act(V("SG", C * m + a, C * m + C), V(pa, a - lo, C - lo), AF.Sign, bias=own, scale=-1.0)
+                act(slot(m + 1, a), V("SG", C * m + a, C * m + C), AF.Relu, scale=-1.0, accum=col("RS", m))
+            else:
+                ts(slot(m + 1, a), V("ps%d" % STAGES[-2][2], 0, C - a) if narrow else V(pv, a - lo, C - lo), own, GT)
+                scan(V("RO", 20 * a + m, 20 * C, 20), V("ONE", a, C), slot(m + 1, a), col("CNT", m)[0], MUL, ADD, col("CNT", m))
+
+    for stage in STAGES[:-1]:
+        compare(*stage)
     for r in range(ROUNDS):
         last = r == ROUNDS - 1
         cw, cwn, qt, st = V("CW", 20 * r, 20 * r + 20), V("CW", 20 * r + 20, 20 * r + 40), "QT%d" % r, "STT%d" % r
-        mm(0, "QU2", "SU2", 0, "QX", "SX", 0, C)
-        mm(1, "QU2", "SU2", 0, "QX", "SX", 0, C)
-        for a, b in ((208, C), (0, 208)):
-            tt(V("M3", a, b), V("ps0", a, b), V("LM", a, b), MIN)
-            scan(V("H3", a, b), V("A3", a, b), V("M3", a, b), 0.0, ADD, MAX)
-        own = [19, 18, 17, 16, 15, 14, 13]
-
-        def sign(i):
-            m = own[i]
-            act(V("SG", C * i, C * i + 16 * m), V("ps1", 0, 16 * m), AF.Sign, bias=col("H3", 16 * m + 15), scale=-1.0)
-
-        def relu(i):
-            m = own[i]
-            o = V("CC", m - 16, 64 * m, 4) if m > 16 else V("CB", m - 13, 64 * m, 4)
-            act(o, V("SG", C * i, C * i + 16 * m), AF.Relu, accum=col("RS", m))
-        sign(0)
-        for i in range(7):
-            if i < 6:
-                sign(i + 1)
-            relu(i)
-        tt(V("CC", 0, 4 * C, 4), V("ps0", 0, C), V("H3"), LE)
-        for m in range(12, 0, -1):
-            c, t = (m - 1) // 4, (m - 1) % 4
-            ts(V("CA", 4 * CH[c] + t, 4 * CH[c] + 64 * m, 4), V("ps0", 0, 16 * m), col("H3", 16 * m + 15), LT)
-            if r == 0 and m == 8:
-                ts(V("NQ2"), V("NQI"), -79.75, MUL)
-                ts(V("CNT"), V("M16"), R_, SUB, 16.0, ADD)
-                cp(cw, V("C0"))
-                tt(V("POS"), V("NBI"), V("NQ2"), ADD)
+        compare(*STAGES[-1])
         if r == 0:
             quant("QB", "SB", 0, 128, V("BL2"))
-        quant("QCC", "SCC", 0, C, V("CC"))
-        mm(2, "QB", "SB", 0, "QCC", "SCC", 0, C, True, False)
-        wa = 448 if r == 0 else 384
-        quant("QCA", "SCA", 0, wa, V("CA", 0, 4 * wa))
-        for c in range(3):
-            mm(2, "QB", "SB", 0, "QCA", "SCA", CH[c], CH[c] + (192 if c == 2 else 128), False, False)
-        scan(V("RD"), V("T16B"), V("CC", 0, 4 * C, 4), 0.0, MIN, ADD)
-        for t in range(4):
-            if t == 1:
-                quant("QCB", "SCB", 0, 256, V("CB"))
-                mm(2, "QB", "SB", 0, "QCB", "SCB", 0, 256, False, True)
-                move("a", V("CS"), V("ps2", 0, C))
-                tt(V("UT"), V("CNT"), V("RD", 15, C, 16), SUB)
-            if t == 3:
-                tt(V("UT", 13, 20), V("UT", 13, 20), V("RS", 13, 20), SUB)
-            scan(V("RO", t, 4 * 384, 4), V("AR"), V("CA", t, 4 * 384, 4), 0.0, MIN, ADD)
-        for c in range(3):
-            e = 4 * (CH[c] + 64 * c + 63)
-            tt(V("UT", 1 + 4 * c, 5 + 4 * c), V("UT", 1 + 4 * c, 5 + 4 * c), V("RO", e, e + 4), SUB)
-        cp(V("UO"), V("UT"))
-        if r == 0:
-            afill(V("AA", 0, 1600, 5), 1e9)
-            afill(V("AA", 1600, 1616), 1000.0)
-            afill(V("M5"), 1.0)
-        tt(V("BYK"), IND(V("TM1"), V("UO")), V("CS"), ADD)
-        aff("a", V("G2", 4, 1600, 5), IND(V("BYK"), cw), 2.0 ** 20, 0.5)
-        cp(V("AA", 4, 1600, 5), IND(V("BYK"), cw))
-        if r == 0:
             for e in range(4):
-                act(V("NALL", e, 100, 5), V("POS", 20 * e, 20 * e + 20), AF.Identity, scale=4.0)
-            act(V("NALL", 4, 100, 5), V("M16"), AF.Identity, bias=R_)
-            act(V("M5", 4, 100, 5), V("NALL", 4, 100, 5), AF.Identity, bias=-1596.0, scale=5.0)
-            move("a", V("HH"), IND(V("W16", 32, 48), V("ORR")))
-        scan(V("ST"), V("G2", 4, 1600, 5), V("ONEF"), 1000.0, MIN, ADD)
+                ts(V("NALL", e, 100, 5), V("POS", 20 * e, 20 * e + 20), 4.0, MUL)
+        ts(V("D16"), IND(V("LR"), col("OS", 0)), 2.0 ** 35, ADD, 2.0 ** 35, SUB)
+        ts(V("ST"), IND(V("LR"), col("OS", 0)), col("D16", 0), SUB)
+        ts(V("EQ"), V("NALL"), col("ST", 0), EQ)
+        scan(V("EQS"), V("EQ"), V("M5"), 0.0, MAX, MUL)
+        ts(V("O1"), V("EQS", 4, 100, 5), 1.0, ADD)
+        for (a, b), q in zip(SPLIT[len(Q_NF)], Q_NF):
+            move(q, V("NFF", 16 * a, 16 * b), IND(V("FT", 0, 2), V("O1", a, b)))
+        for (a, b), q in zip(SPLIT[len(Q_NF)], Q_NF):
+            move(q, V("NFC", 16 * a, 16 * b), IND(V("NFF"), V("OP", a, b)))
+        for k in TILES:
+            quant("QC", "SQC", C * k + Q0[k], C * k + C, V("CT", 4 * (C * k + Q0[k]), 4 * (C * k + C)))
+            mm(4, "QB", "SB", 0, "QC", "SQC", C * k, C * k + C, k == TILES[0], k == TILES[-1])
+        scan(V("RD"), V("T16B"), slot(0, 0), 0.0, MIN, ADD)
+        tt(V("UT"), V("RO", 20 * C - 20, 20 * C), V("RD", 15, C, 16), ADD)
+        tt(V("UT"), V("UT"), V("RS"), ADD)
+        if r == 0:
+            move("a", V("HHB"), V("HH"))
+        ts(V("US"), V("UT"), 160.0, ADD, SC, MUL)
+        scan(V("HC"), V("HH"), V("ps4", 0, C), 0.0, MUL, ADD)
+        tt(V("UB"), V("US"), V("HC", 15, C, 16), SUB)
+        ts(V("BC"), V("UB"), ISC, MUL)
+        scatter(V("SF", 16, 336), V("BC"), V("NFC"))
+        aff("a", V("BYC"), IND(V("T3"), V("BC")), 1.0, -160.0)
+        move("a", V("BYF"), IND(V("BYC"), cw))
+        scan(V("HB"), V("HHB"), V("BYF"), 0.0, MUL, ADD)
+        aff(Q_SD, V("SD"), V("SF", 15, 335), -1.0 - EPS, 1.0)
+        ts(V("BF"), V("HB", 15, C, 16), ISC, MUL, 160.0, ADD)
+        scan(V("K1S"), V("SD"), V("SF", 16, 336), -161.0, ADD, ADD)
+        scan(V("D0S"), V("SF", 16, 336), V("ONE", 0, C), -160.0 * INF, ADD, MUL)
+        for (a, b), q in zip(SPLIT[len(Q_K1)], Q_K1):
+            aff(q, V("K1", 16 * a, 16 * b), IND(V("K1S"), V("BF", a, b)), 1.0, 161.0)
+        act(T1, col("D0S", C - 1), AF.Relu, scale=EPS, bias=96.0)
+        aff("e", RR_, T1, 1.0, 64.0)
+        for (a, b), q in zip(SPLIT[len(Q_AA)], Q_AA):
+            aff(q, V("AA", 80 * a + 4, 80 * b, 5), IND(V("D0S"), V("BF", a, b)), EPS, 480.0)
+        aff(Q_R, NEGA, T1, -1.01 * EPS, -78.64 * EPS)
+        aff(Q_R, S3, T1, -EPS, -68.0 * EPS)
+        aff(Q_R, B3, T1, 320.0 * EPS, 1.0 + 320.0 * 68.0 * EPS)
         if r == 0:
             ts(V("N1"), V("POS"), 4.0, MUL)
-        ts(V("EQ"), V("NALL"), col("ST", C - 1), ADD, 320.5, EQ)
-        scan(V("EQS"), V("EQ"), V("M5"), 0.0, MAX, MUL)
-        ts(V("O1"), V("EQS", 4, 100, 5), 1600.0, ADD)
-        cp(V("K1"), IND(V("AA"), V("O1")))
-        step("G2", "K2", V("K1"), "N1", 320.0, 1.0)
-        if not last:
-            aff("a", V("C4"), IND(V("T3", 0, C), cw), 4.0, 0.0)
 
-        def unplaced():
-            if r == 0:
-                ts(V("C2"), V("C0"), 2.0, MUL, 321.0, ADD)
-                ts(V("N5"), V("POS"), 20.0, MUL, 4.0, ADD)
-            ts(V("Y1"), V("HOR", 15, C, 16), ISC, MUL, -200000.0, ADD)
-            tt(V("T2"), V("Y1"), V("C2"), MIN)
-        count_pass("K2", unplaced)
-        tt(V("PM"), V("PL"), V("T2"), MAX)
-        ts(V("O2"), V("PM"), 319.0, ADD, 0.5, MUL)
-        cp(V("CAP"), IND(V("T3"), V("O2")))
-        move("a", V("G3", 4, 1600, 5), IND(V("T3"), V("O2")))
-        step("G3", "K3", V("CAP"), "N1", 320.0, 320.0)
-        aff("a", V("G4", 4, 1600, 5), V("CAP"), 256.0, -SH - 256.0 * 320)
-        step("G4", "K4", V("K3"), "N5", 320.0, 320.0 - SH)
-        count_pass("K4")
-        ts(cwn, V("PL"), -0.5, MUL, 159.5, ADD)
-        lr, c4 = IND(V("LR"), cwn), V("C4L" if last else "C4")
-        op("v", lambda: g.vector.tensor_copy(lr[0], c4[0]), reg(c4, cwn), V("LR")[1])
+        def cap(a, b):
+            move("e", V("G", 80 * a + 4, 80 * b, 5), V("K1", 16 * a, 16 * b))
+        step(PARTS, "AA", "G", "K2", 5, V("K1"), "N1", RR_, ADD, MIN, before=cap)
+        for a, b in HALVES:
+            aff("a", V("F3", 16 * a, 16 * b), V("AA", 80 * a + 4, 80 * b, 5), S3, B3)
+            aff("a", V("AB", 112 * a + 4, 112 * b, 7), V("AA", 80 * a + 4, 80 * b, 5), -EPS, 1.0 + 320.0 * EPS)
+        if r == 0:
+            ts(V("N5"), V("POS"), 20.0, MUL, 4.0, ADD)
+            unplaced(cw)
+
+        def spread(a, b):
+            act(V("EX", 16 * a, 16 * b), V("K3", 80 * a + 3, 80 * b, 5), AF.Exp, scale=NEGA, bias=TOP)
+        step(PARTS3, "AA", "G", "K3", 5, V("K2"), "N5", RR_, ADD, MIN, after=spread)
+        for a, b, _ in PARTS3:
+            tt(V("E3", 16 * a, 16 * b), V("EX", 16 * a, 16 * b), V("F3", 16 * a, 16 * b), MUL)
+        for a, b in HALVES:
+            act(V("G4", 112 * a + 4, 112 * b, 7), V("K3", 80 * a + 4, 80 * b, 5), AF.Relu, scale=-2.0 ** 89, bias=CAPB)
+        step(PARTS4, "AB", "G4", "K4", 7, V("E3"), "N1", None, MUL, MAX, after=count_early)
+        count_pass(20 * r + 20)
+        scatter(V("LR"), cwn, V("PK"))
         if last:
-            move("a", V("CN"), IND(V("T3", 0, C), cwn))
-            for e in range(3):
+            move("a", V("CN"), IND(V("T3"), cwn))
+            for e in range(2):
                 names_of(e)
+        else:
+            unplaced(cwn)
         scan(V("HL"), V("HH"), V("LR"), 0.0, MUL, ADD)
         order = (1, 0, 3, 2)
-        if last:
-            ts(V("VI"), V("HL", 15, C, 16), ISC, MUL)
-            ts(V("LO"), V("VI"), 2047, AND)
-            for t in order:
-                ts(V("OT", 20 * t, 20 * t + 20), V("LO"), float(t), ADD)
-        else:
-            for t in order:
-                ts(V("OT", 20 * t, 20 * t + 20), V("HL", 15, C, 16), ISC, MUL, float(t), ADD)
-        for t in order:
-            move("a" if t % 2 else "v", V("TT", 1024 + t, 1280, 4), IND(xw, V("OT", 20 * t + 16, 20 * t + 20)))
-        quant(qt, st, 320, 448, V("TT", 1024, 1536))
-        for e in set(wr[qt][320:384]):
-            need("g", e[0], e[1])
-        g.remote_dma(T[qt][:, 0:KB].bitcast(dt.uint8), T[qt][:, 320:384].bitcast(dt.uint8), T.sem["arr%d" % r], T.sem.sent, pid, rid, emask)
-        g.remote_dma(T[st][:, 0:KB], T[st][:, 320:384], T.sem["arr%d" % r], T.sem.sent, pid, rid, emask)
-        for n in (qt, st):
-            wr[n][0:KB] = [("arr%d" % r, 2 * neng)] * KB
-        for t in order:
-            move("a" if t % 2 else "v", V("TT", t, 1024, 4), IND(xw, V("OT", 20 * t, 20 * t + 16)))
-        quant(qt, st, 64, 320, V("TT", 0, 1024))
-        if r == 0:
-            quant("QE", "SE", 0, 512, V("EB"))
-        for b in range(4):
-            mm(b, "QE", "SE", 128 * b, qt, st, 128, 384, True, False)
-            mm(b, "QE", "SE", 128 * b, qt, st, 64, 320, False, True)
-        for b in range(4):
-            mm(4 + b, "QE", "SE", 128 * b, qt, st, 64, 192, True, False)
-        for b in range(4):
-            mm(4 + b, "QE", "SE", 128 * b, qt, st, 0, 128, False, True)
-        if last:
-            ts(V("HI"), V("VI"), 11, SHR)
-            names_of(3)
-            cp(V("OP"), V("HI"))
-            quant("QV", "SV", 0, 128, V("Vb"))
-            names_out("a", 0)
-        else:
-            ts(V("C2"), V("PL"), -1.0, MUL, 640.0, ADD)
-            if r == ROUNDS - 2:
-                tt(V("C4L"), IND(V("T4"), cwn), V("I2K"), ADD)
-        evac((0, 1, 2, 3), "ZS", 128, 256, 0, False)
-        quant("QZ", "SZ", 128, 384, V("ZS", 512, 1536))
-        for b in range(4):
-            mm(b, "QW", "SW", 128 * b, "QZ", "SZ", 128, 384)
-        evac((4, 5, 6, 7), "ZS", 64, 64, 0, False)
-        quant("QZ", "SZ", 0, 128, V("ZS", 0, 512))
-        for b in range(4):
-            mm(4 + b, "QW", "SW", 128 * b, "QZ", "SZ", 0, 128)
-        evac((0, 1, 2, 3), "XS", 64, 256, 0, True)
-        evac((4, 5, 6, 7), "XS", 0, 64, 64, True)
-        quant("QX", "SX", 0, C, xw)
 
-    mm(0, "QV", "SV", 0, "QX", "SX", 0, C)
-    dma("s", T.oc[:, :], bits(V("QX")), V("QX")[1], [])
-    names_out("a", 1)
-    names_out("v", 2)
-    cp(V("YS"), V("ps0", 0, C))
+        def take(t, a, b):
+            move(TAKE[t], V("TT", 4 * a + t, 4 * b, 4), IND(xw, V("OT", 20 * t + a // 16, 20 * t + b // 16)))
+        for t in order:
+            ts(V("OT", 20 * t, 20 * t + 20), V("HL", 15, C, 16), ISC4, MUL, float(t), ADD)
+        for a, b in TAKES:
+            for t in order:
+                take(t, a, b)
+            top = max(b, a + 128)
+            quant(qt, st, KB + a, KB + top, V("TT", 4 * a, 4 * top))
+            if b == C:
+                send(r)
+        ts(V("VI"), V("HL", 15, C, 16), ISC, MUL)
+        ts(V("HI"), V("VI"), 4095, AND)
+        cp(V("OP"), V("HI"))
+        if last:
+            for e in (2, 3):
+                names_of(e)
+            for e in range(4):
+                names_out("e", e)
+            dma("s", T.on[:, :], T.ONB[0:128:16, :], V("ONB")[1], [])
+            quant("QV", "SV", 0, 128, V("Vb"))
+        else:
+            pack(20 * r + 20)
+        for lo, hi, pb, sb in PIECES:
+            top = max(hi, lo + 128)
+            for b in range(4):
+                mm(pb + b, "QE", "SE", 128 * b, qt, st, KB + lo, KB + top, True, False)
+                mm(pb + b, "QE", "SE", 128 * b, qt, st, lo, top, False, True)
+            for b in range(4):
+                evac(b, pb + b, "ZS", lo, hi - lo, False)
+            quant("QZ", "SZ", lo, top, V("ZS", 4 * lo, 4 * top))
+            for b in range(4):
+                mm(pb + b, "QW", "SW", 128 * b, "QZ", "SZ", lo, top)
+            for b in range(4):
+                evac(b, pb + b, "XS", lo, hi - lo, True)
+            quant("QX", "SX", lo, top, V("XS", 4 * lo, 4 * top))
+            if last:
+                mm(sb, "QV", "SV", 0, "QX", "SX", lo, top)
+                dma("s", T.oc[:, 4 * lo:4 * hi], bits(V("QX", lo, hi)), V("QX", lo, hi)[1], [])
+                move("e", V("YS", lo, hi), V("ps%d" % sb, 0, hi - lo))
+                dma("s", T.y[:, lo:hi], V("YS", lo, hi)[0], V("YS", lo, hi)[1], [])
+            else:
+                for stage in STAGES[:-1]:
+                    if stage[0] == lo:
+                        compare(*stage)
     for k in range(4):
-        dma("s", T.osc[4 * k:4 * k + 4, :], T.SX[32 * k:32 * k + 4, 0:C], V("SX")[1], [])
-    names_out("a", 3)
-    dma("s", T.y[:, :], V("YS")[0], V("YS")[1], [])
-    dma("a", T.on[:, :], T.ONB[0:128:16, :], V("ONB")[1], [])
+        dma("s" if k % 2 else "a", T.osc[4 * k:4 * k + 4, :], T.SX[32 * k:32 * k + 4, 0:C], V("SX")[1], [])
+    issue()
     for sem in sorted(count):
         need("g", sem, count[sem])
     g.wait_ge(T.sem.sent, 2 * neng * ROUNDS)

from concourse.mybir import dt, AluOpType, AxisListType, ActivationFunctionType

C, KB, ROUNDS = 320, 64, 3
NA = 13
NE = 6
NH = 0
ND = 20 - NA
PIECES = ((128, 320, 0, 0), (0, 128, 4, 2))
PARTS = ((0, 14, 2), (14, 20, 0))
PARTS3 = ((0, 12, 2), (12, 20, 0))
PARTS4 = ((0, 10, 2), (10, 20, 1))
BIG = 1e28
P60 = 2.0 ** 60
INF = 2.0 ** 23
EPS = 2.0 ** -23
TOP = 75.5
F32, BF, I32, U16, Q4, U8 = "float32", "bfloat16", "int32", "uint16", "float8_e4m3fn_x4", "uint8"
Q0 = (0, 64, 128, 192, 192)
STAGES = ((128, 320, 0), (0, 128, 2))
AHEAD = False
TAKES = ((128, 320), (0, 128))
HALVES = ((0, 20),)
SPLIT = {1: ((0, 20),), 2: ((0, 10), (10, 20))}
Q_SD, Q_K1, Q_AA, Q_NF, Q_R = "v", "v", "e", "a", "a"
FREE = "av"
EVAC = "eeee"
TAKE = "eeee"
CALL_V, CALL_A, CALL_P, CALL_D, PE, LEAST = 20.0, 20.0, 20.0, 600.0, 0.5, 64.0
CYCLE, GATHER, SCATTER, WAKE, LEAN = 0.85, 1.8, 5.0, (120.0, 260.0), (0.0, 0.0, 50.0, 50.0)
RING = (3000.0, 1800.0, 1800.0)
RUNS = "aaaavvvv" + "aaaaaavvvvv"
TILES = (4, 3, 2, 0, 1)

_S = {
    "XS": (BF, 4 * C), "ZS": (BF, 4 * C), "TT": (BF, 4 * (C + KB)), "QX": (Q4, C), "SX": (U8, C),
    "QZ": (Q4, C), "SZ": (U8, C), "QW": (Q4, 512), "SW": (U8, 512),
    "Ub": (BF, 512), "QU": (Q4, 128), "SU": (U8, 128), "QU2": (Q4, 128), "SU2": (U8, 128),
    "Vb": (BF, 512), "QV": (Q4, 128), "SV": (U8, 128),
    "ONE": (BF, 516), "BL1": (BF, 512), "BL2": (BF, 512), "QB": (Q4, 128), "SB": (U8, 128),
    "EB": (BF, 1032), "QE": (Q4, 512), "SE": (U8, 512),
    "NBI": (I32, 80), "O16I": (I32, 8), "O16": (U16, 8), "ORR": (U16, 20), "W16": (F32, 128),
    "T16B": (BF, C), "HH": (F32, C), "HHB": (BF, C), "LM": (F32, C), "A3": (F32, C), "Z16": (F32, C),
    "APS": (BF, C * ND), "T3": (F32, C), "T4K": (F32, C),
    "M3": (F32, C), "H3": (F32, C), "RD": (BF, C), "CT": (BF, 5 * 4 * C), "QC": (Q4, 5 * C), "SQC": (U8, 5 * C), "ZT": (BF, 4 * 192),
    "RO": (BF, 20 * C), "SG": (BF, 20 * C), "RM": (F32, C), "NFF": (BF, C), "NFC": (BF, C), "HC": (F32, C),
    "SF": (BF, 336), "SD": (BF, C), "K1S": (BF, C), "D0S": (BF, C), "BYC": (BF, C), "BYF": (BF, C), "HB": (BF, C),
    "AA": (F32, 5 * C), "AB": (F32, 7 * C), "K1": (F32, C), "G": (F32, 5 * C), "G4": (F32, 7 * C),
    "K2": (F32, 5 * C), "K3": (F32, 5 * C), "K4": (F32, 7 * C), "EX": (F32, C), "F3": (F32, C), "E3": (F32, C),
    "HOR": (F32, C), "JK": (BF, C * NA), "CMP": (BF, C * ND), "CMS": (BF, C * ND),
    "CMH": (BF, 1280), "CMG": (BF, 1280), "APH": (BF, 1280),
    "PK": (F32, C), "LR": (F32, C), "HL": (F32, C), "CN": (F32, C), "RR": (F32, 4 * C), "ONB": (F32, 4 * C), "YS": (F32, C),
}
_SMALL = {
    F32: (("NQ", 80), ("NQ2", 80), ("POS", 80), ("NALL", 100), ("M5", 100), ("EQ", 100), ("EQS", 100), ("CF", 16), ("I16", 16),
          ("D16", 16), ("M16", 20), ("M4", 20), ("CNT", 20), ("C0", 20), ("RS", 20), ("UT", 20), ("US", 20), ("UB", 20), ("PL", 20),
          ("SC", 16), ("ST", 16), ("FT", 8), ("P0", 20), ("P2", 20)),
    I32: (("NQI", 80), ("PI", 8), ("CI", 8), ("VI", 20), ("HI", 20)),
    U16: (("N1", 80), ("N5", 80), ("OS", 2), ("O1", 20), ("BC", 20), ("BF", 20), ("CW", 80), ("OT", 80), ("OP", 20)),
}
_AT = {k: (k, 0, v[1]) for k, v in _S.items()}
for _d, _l in _SMALL.items():
    _n = 0
    for _k, _w in _l:
        _AT[_k] = ("pool_" + _d, _n, _w)
        _n += (_w + 15) // 16 * 16
    _S["pool_" + _d] = (_d, _n)
for _r in range(ROUNDS):
    for _k, _d in (("QT%d" % _r, Q4), ("STT%d" % _r, U8)):
        _S[_k] = (_d, C + 2 * KB)
        _AT[_k] = (_k, 0, C + 2 * KB)
SCRATCH = {k: ("sbuf", [128, v[1]], v[0]) for k, v in _S.items()}
for _b in range(8):
    SCRATCH["ps%d" % _b] = ("psum", [128, 512], F32)
    _AT["ps%d" % _b] = ("ps%d" % _b, 0, 512)
NDMA, LOADS = 32, 10
SEMAPHORES = ["qv", "qa", "qp", "qg", "sent"] + ["arr%d" % r for r in range(ROUNDS)] + ["d%d" % i for i in range(NDMA)]

ADD, SUB, MUL, MAX, MIN = AluOpType.add, AluOpType.subtract, AluOpType.mult, AluOpType.max, AluOpType.min
LT, LE, EQ, NEQ = AluOpType.is_lt, AluOpType.is_le, AluOpType.is_equal, AluOpType.not_equal
GT = AluOpType.is_gt
AND, SHR = AluOpType.bitwise_and, AluOpType.arith_shift_right
AF = ActivationFunctionType


def rank_program(g, core, T, topo):
    rank = T.rank_of(core)
    if rank is None:
        return
    nxt = T.cores[(rank + 1) % len(T.cores)]
    rid, pid = topo.addr(nxt, core)
    emask = topo.mask(core, nxt)
    neng = len(topo.engines(core, nxt))

    Q = {"v": g.vector, "a": g.scalar, "p": g.tensor, "g": g, "s": g.sync}
    count, known, clock = {}, {q: {} for q in Q}, {}
    wr = {k: [None] * v[1] for k, v in _S.items()}
    rd = {k: [] for k in _S}
    bank = {"ps%d" % b: [None, [], []] for b in range(8)}
    ndma, ops = [0], []

    def V(name, a=0, b=None, s=1):
        buf, at, n = _AT[name]
        a, b = at + a, at + (n if b is None else b)
        return (T[buf][:, a:b] if s == 1 else T[buf][:, a:b:s], [(buf, a, b, s)])

    def col(name, j):
        return V(name, j, j + 1)

    def IND(win, off):
        return (win[0].indirect(off[0]), win[1] + off[1])

    def need(q, sem, val):
        if known[q].get(sem, 0) >= val:
            return
        Q[q].wait_ge(T.sem[sem], val)
        for s2, v2 in clock.get((sem, val), {}).items():
            if known[q].get(s2, 0) < v2:
                known[q][s2] = v2
        known[q][sem] = val

    def op(q, call, reads, writes, cost, after=0.0, event=None, acc=False):
        me, deps, behind = len(ops), set(), set()
        for n in set(r[0] for r in reads + writes if r[0] in bank):
            k = bank[n]
            if k[0] != q or q == "e":
                k[0], k[1], k[2] = q, [], k[1]
            deps.update(k[2])
            if q == "p":
                (behind if acc else deps).update(k[1][-1:])
            k[1].append(me)
        for n, a, b, s in reads + writes:
            if n not in bank:
                deps.update(wr[n][a:b:s])
        for n, a, b, s in writes:
            if n not in bank:
                mine, keep = set(range(a, b, s)), []
                for o2, a2, b2, cells in rd[n]:
                    if a2 < b and a < b2 and not mine.isdisjoint(cells):
                        deps.add(o2)
                        if cells <= mine:
                            continue
                    keep.append((o2, a2, b2, cells))
                rd[n] = keep
        for n, a, b, s in reads:
            if n not in bank:
                rd[n].append((me, a, b, set(range(a, b, s))))
        for n, a, b, s in writes:
            if n not in bank:
                wr[n][a:b:s] = [me] * len(range(a, b, s))
        if event == "dma" and len(ops) < LOADS:
            behind.update(i for i, o in enumerate(ops) if o[0] == q)
        deps.discard(None)
        deps.discard(me)
        ops.append((q, call if q == "e" else {q: call}, deps, behind, cost if q == "e" else {q: cost}, after, event))

    def issue():
        n = len(ops)
        before, behind, done = [[] for _ in ops], [[] for _ in ops], [None] * n
        for i, o in enumerate(ops):
            for d in o[2] | o[3]:
                lag = (ops[d][5], True) if d in o[2] else (0.0, False)
                before[i].append((d,) + lag)
                behind[d].append((i,) + lag)

        def place(order, links, tail, lean):
            ends, busy, at = [0.0] * n, {q: [] for q in Q}, [None] * n
            for i in order:
                best = None
                for q, cost in ops[i][4].items():
                    t, line, k = max([ends[d] + lag + (WAKE[at[d][1] != q] if wait else 0.0) for d, lag, wait in links[i]]
                                     + [ops[i][5] if tail else 0.0]), busy[q], 0
                    while k < len(line) and line[k][0] < t + cost:
                        t = max(t, line[k][1])
                        k += 1
                    if best is None or t + cost + lean < best[0]:
                        best = (t + cost, t, q, k)
                busy[best[2]].insert(best[3], (best[1], best[0]))
                ends[i], at[i] = best[0], best[1:3]
            return ends, at
        ends, at = kept = place(range(n), before, False, LEAN[0])
        for lean in LEAN:
            back = place(sorted(range(n), key=lambda i: (-ends[i] - ops[i][5], -i)), behind, True, lean)[0]
            ends, at = place(sorted(range(n), key=lambda i: (-back[i], i)), before, False, lean)
            if max(e + o[5] for e, o in zip(ends, ops)) < max(e + o[5] for e, o in zip(kept[0], ops)):
                kept = ends, at
        for k in sorted(range(n), key=lambda i: (kept[1][i][0], i)):
            q = kept[1][k][1]
            deps = {}
            for d in ops[k][2]:
                deps[done[d][0]] = max(deps.get(done[d][0], 0), done[d][1])
            for sem in sorted(deps, key=lambda x: (-len(clock.get((x, deps[x]), {})), x)):
                need(q, sem, deps[sem])
            event = ops[k][6]
            if event is None or event == "dma":
                sem, inc = ("q" + q, 1) if event is None else ("d%d" % ndma[0], 16)
                ndma[0] += event == "dma"
                ops[k][1][q]().then_inc(T.sem[sem], inc)
                count[sem] = count.get(sem, 0) + inc
                done[k] = (sem, count[sem])
                clock[done[k]] = dict(known[q])
            else:
                ops[k][1][q]()
                done[k] = event

    def val(x):
        return x[0] if isinstance(x, tuple) else x

    def reg(*xs):
        return [r for x in xs if isinstance(x, tuple) for r in x[1]]

    def size(v):
        n, a, b, s = v[1][0]
        return len(range(a, b, s))

    def cycles(o, i, *more, rate=1.0):
        if len(i[1]) > 1:
            return 60.0 + CYCLE * GATHER * size(o)
        if i[1][0][0] in bank:
            return CALL_P + CYCLE * max(LEAST, size(o))
        if rate is None:
            return CALL_A + CYCLE * max(LEAST, size(o))
        if all(x[1][0][0] in _S and _S[x[1][0][0]][0] in (BF, U16) for x in (o, i) + more):
            rate *= 0.5
        return CALL_V + CYCLE * max(LEAST, rate * size(o))

    def cp(o, i):
        op("v", lambda: g.vector.tensor_copy(o[0], i[0]), i[1], o[1], cycles(o, i))

    def ts(o, i, s1, o0, s2=None, o1=None):
        if o1 is None:
            op("v", lambda: g.vector.tensor_scalar(o[0], i[0], val(s1), None, o0), reg(i, s1), o[1], cycles(o, i))
        else:
            op("v", lambda: g.vector.tensor_scalar(o[0], i[0], val(s1), val(s2), o0, o1), reg(i, s1, s2), o[1], cycles(o, i))

    def tt(o, a, b, o0):
        op("v", lambda: g.vector.tensor_tensor(o[0], a[0], b[0], o0), reg(a, b), o[1], cycles(o, a, b, rate=1.0 if a[1][0][0] in bank else 2.0))

    def scan(o, d0, d1, init, o0, o1, start=None):
        op("v", lambda: g.vector.tensor_tensor_scan(o[0], d0[0], d1[0], init, o0, o1), reg(d0, d1, start), o[1], cycles(o, d0, d1))

    def scatter(win, off, src):
        o = IND(win, off)
        op("v", lambda: g.vector.tensor_copy(o[0], src[0]), reg(src, off), win[1], 50.0 + CYCLE * SCATTER * size(src))

    def fill(o, c):
        op("v", lambda: g.vector.memset(o[0], c), [], o[1], cycles(o, o))

    def quant(qc, qs, a, b, src):
        c, s = V(qc, a, b), V(qs, a, b)
        op("v", lambda: g.vector.quantize_mx(c[0], s[0], src[0]), src[1], c[1] + s[1], 30.0 + 0.225 * size(src))

    def act(o, i, f, bias=0.0, scale=1.0, accum=None, more=0.0):
        if accum is None:
            op("a", lambda: g.scalar.activation(o[0], i[0], f, bias=val(bias), scale=val(scale)), reg(i, bias, scale), o[1],
               cycles(o, i, rate=None) + more)
        else:
            op("a", lambda: g.scalar.activation(o[0], i[0], f, bias=val(bias), scale=val(scale), accum_out=accum[0]),
               reg(i, bias, scale), o[1] + accum[1], cycles(o, i, rate=None) + 20.0)

    def afill(o, c):
        n, a, b, s = o[1][0]
        act(o, V("ONE", 0, len(range(a, b, s))), AF.Identity, scale=float(c))

    def either(o, i, on_a, on_v, reads):
        op("e", {"a": on_a, "v": on_v}, reads, o[1], {"a": cycles(o, i, rate=None) + 15.0 * (len(i[1]) > 1), "v": cycles(o, i)})

    def aff(q, o, i, scale, bias):
        if q == "a":
            act(o, i, AF.Identity, bias=bias, scale=scale)
        elif q == "v":
            ts(o, i, scale, MUL, bias, ADD)
        else:
            either(o, i, lambda: g.scalar.activation(o[0], i[0], AF.Identity, bias=val(bias), scale=val(scale)),
                   lambda: g.vector.tensor_scalar(o[0], i[0], val(scale), val(bias), MUL, ADD), reg(i, scale, bias))

    def move(q, o, i):
        if q == "a":
            op("a", lambda: g.scalar.activation(o[0], i[0], AF.Copy), i[1], o[1], cycles(o, i, rate=None))
        elif q == "v":
            cp(o, i)
        else:
            either(o, i, lambda: g.scalar.activation(o[0], i[0], AF.Copy), lambda: g.vector.tensor_copy(o[0], i[0]), i[1])

    def mm(b, lq, ls, la, rq, rs, ra, rb, start=True, stop=True):
        o, l1, l2, r1, r2 = V("ps%d" % b, 0, rb - ra), V(lq, la, la + 128), V(ls, la, la + 128), V(rq, ra, rb), V(rs, ra, rb)
        op("p", lambda: g.tensor.matmul_mx(o[0], l1[0], l2[0], r1[0], r2[0], start, stop), reg(l1, l2, r1, r2), o[1],
           20.0 + PE * (rb - ra + 16), after=60.0, acc=not start)

    def iota(o, pat, base, cm=0, small=True):
        if small:
            op("g", lambda: g.iota(o[0], pat, base, cm, allow_small_or_imprecise_dtypes=True), [], o[1], 160.0 + 3.5 * CYCLE * size(o))
        else:
            op("g", lambda: g.iota(o[0], pat, base, cm), [], o[1], 160.0 + 3.5 * CYCLE * size(o))

    def sel(o, i, pat, cmpop, base, cm):
        op("g", lambda: g.affine_select(o[0], i[0], pat, cmpop, 0.0, base, cm), i[1], o[1], 210.0 + 3.5 * CYCLE * size(o))

    def dma(q, o, i, reads, writes, lands=2000.0):
        op(q, lambda: Q[q].dma_start(o, i), reads, writes, CALL_D, after=lands, event="dma")

    def send(r):
        qt, st, arr = "QT%d" % r, "STT%d" % r, T.sem["arr%d" % r]

        def calls():
            g.remote_dma(T[qt][:, 0:KB].bitcast(dt.uint8), T[qt][:, C:C + KB].bitcast(dt.uint8), arr, T.sem.sent, pid, rid, emask)
            g.remote_dma(T[st][:, 0:KB], T[st][:, C:C + KB], arr, T.sem.sent, pid, rid, emask)
        op("g", calls, reg(V(qt, C, C + KB), V(st, C, C + KB)), reg(V(qt, 0, KB), V(st, 0, KB)), 600.0, after=RING[r], event=("arr%d" % r, 2 * neng))

    def bits(v):
        return v[0].bitcast(dt.uint8)

    xw = V("XS")
    dma("a", V("Ub")[0], T.u[:, :], [], V("Ub")[1])
    for k, (a, b) in enumerate(TAKES):
        dma("s", V("XS", 4 * a, 4 * b)[0], T.x[:, 4 * a:4 * b], [], V("XS", 4 * a, 4 * b)[1], 2700.0 + 1000.0 * k)
    for e in range(4):
        d = V("NBI", 20 * e, 20 * e + 20)
        dma("s", d[0], T.nb[e:128:4, :], [], d[1], 4000.0)
    for o, i, d in ((bits(V("QW")), T.wc, V("QW")), (V("SW")[0], T.ws, V("SW")), (V("Vb")[0], T.v, V("Vb"))):
        dma("s", o, i[:, :], xw[1], d[1])

    R_, SC, ISC, CB_, ISC4, ISCK, R4, CAPB = (col("CF", j) for j in (0, 1, 3, 4, 8, 9, 10, 11))
    CST, CUP, RR_, S3, B3, T1, T2, NEGA, TOPS, CAD = (col("SC", j) for j in range(10))
    fill(V("ONE"), 1.0)
    iota(col("PI", 0), [[0, 1]], 0, 1, small=False)
    iota(V("I16"), [[1, 16]], 0)
    iota(V("M16"), [[16, 20]], 0)
    iota(V("O16I"), [[16, 8]], 0, small=False)
    iota(V("M4"), [[4, 20]], 0)
    iota(V("P0"), [[1, 4], [64, 5]], 0)
    fill(V("AA", 0, 400), 0.0)
    sel(V("BL1"), V("ONE", 0, 512), [[-16, 8], [0, 64]], AluOpType.is_ge, 0, 1)
    sel(V("BL2"), V("BL1"), [[16, 8], [0, 64]], AluOpType.is_ge, 15, -1)
    iota(V("LR"), [[1, 4], [4, 80]], 0)
    iota(V("T16B"), [[0, 20], [1, 16]], 0)
    iota(V("T3"), [[1, C]], 0)
    iota(V("AB", 0, 560), [[0, 560]], 1)
    iota(V("AB", 0, 560, 7), [[0, 80]], 0)
    iota(V("APS", 0, C), [[1, C]], -160)
    iota(V("G4", 6, 7 * C, 7), [[0, C]], 0)
    sel(V("Z16"), V("ONE", 0, C), [[0, 20], [1, 16]], NEQ, 0, 0)
    for b in (2, 3):
        sel(V("EB", 516 * (b - 2), 516 * (b - 1)), V("ONE"), [[-1, 516]], EQ, b, 4)
    for q in range(4):
        iota(V("PK", q, C, 4), [[4100, 80]], 327681 * q)
    iota(V("T4K"), [[4096, C]], 0)
    for b in range(4):
        a = 516 * (b % 2) + 2 * (b < 2)
        quant("QE", "SE", 128 * b, 128 * b + 128, V("EB", a, a + 512))

    def repeat(name, w):
        for a in range(w, _AT[name][2], w):
            dma("s", V(name, a, a + w)[0], V(name, 0, w)[0], V(name, 0, w)[1], V(name, a, a + w)[1], 3000.0)
    act(V("AA", 0, 400, 5), V("ONE", 0, 80), AF.Exp, scale=28.0, more=1300.0)
    repeat("AA", 400)
    repeat("APS", C)
    ts(col("CI", 0), col("PI", 0), 15, AND)
    ts(col("CI", 1), col("PI", 0), 3, AND)
    cp(R_, col("CI", 0))
    ts(V("W16", 16, 32), V("I16"), 0.0, EQ, 2 * BIG, MUL)
    ts(V("D16"), V("I16"), R_, SUB)
    ts(V("ORR"), V("M16"), 0.0, MUL, R_, ADD)
    ts(V("W16", 48, 64), V("D16"), 0.0, EQ, 0.5, SUB)
    ts(col("CI", 2), col("CI", 0), 2, SHR)
    ts(V("W16", 0, 16), V("W16", 48, 64), -2 * BIG, MUL)
    cp(V("O16"), V("O16I"))
    move("a", V("LM"), IND(V("W16", 0, 16), V("ORR")))
    move("a", V("A3"), IND(V("W16", 16, 32), V("ORR")))
    ts(V("W16", 64, 80), V("D16"), 1.0, EQ, P60, MUL)
    ts(V("W16", 80, 96), V("D16"), 0.0, NEQ)
    ts(V("W16", 96, 112), V("D16"), 0.0, EQ)
    move("e", V("AB", 6, 560, 7), IND(V("W16", 96, 112), V("ORR", 0, 5)))
    repeat("AB", 560)
    cp(V("CF", 5, 7), V("CI", 1, 3))
    ts(SC, R_, 15.0, LT, P60, MUL)
    ts(col("CF", 7), R_, 15.0, EQ)
    tt(V("W16", 32, 48), V("W16", 64, 80), V("W16", 80, 96), MAX)
    ts(CB_, col("CF", 5), 80.0, MUL, col("CF", 6), ADD)
    ts(SC, SC, 1.0, MAX)
    ts(ISC, col("CF", 7), 1.0 / P60, MAX)
    ts(R4, R_, 4.0, MUL)
    ts(V("FT", 0, 2), V("I16", 0, 2), INF, MUL)
    ts(CAPB, col("I16", 1), INF - 1024.0, MUL, 2.0 ** 89, MUL)
    fill(V("M5"), 1.0)
    fill(V("SF"), 0.0)
    ts(ISC4, ISC, 2.0 ** -10, MUL)
    ts(V("OP"), V("P0"), R4, ADD)
    fill(V("M5", 4, 100, 5), -1.0)
    ts(V("NALL", 4, 100, 5), V("M16"), R_, ADD)
    ts(V("C0"), V("M4"), CB_, ADD)
    ts(V("CNT"), V("M16"), R_, ADD, -160.0, ADD)
    cp(V("CW", 0, 20), V("C0"))
    fill(V("RS"), 0.0)
    cp(V("RO", 20 * C - 20, 20 * C), V("CNT"))
    fill(V("ZT"), 0.0)

    quant("QU", "SU", 0, 128, V("Ub"))
    o16 = V("O16")
    op("v", lambda: g.vector.tensor_copy(T.QU2[:, 0:128].bitcast(dt.uint32), T.QU[:, 0:128].bitcast(dt.uint32).indirect(o16[0])),
       reg(V("QU"), o16), V("QU2")[1], cycles(V("QU2"), IND(V("QU"), o16)))
    cp(V("SU2"), IND(V("SU"), o16))
    for k in (4, 3, 2, 1, 0):
        afill(V("CT", 4 * (C * k + Q0[k]), 4 * (C * k + min(64 * k + 48, C - 16))), 0.0)
    move("a", V("HH"), IND(V("W16", 32, 48), V("ORR")))
    for k in (4, 3):
        quant("QC", "SQC", C * k, C * k + 192, V("ZT"))
    for a, b in TAKES:
        quant("QX", "SX", a, b, V("XS", 4 * a, 4 * b))
    for k in (2, 1):
        quant("QC", "SQC", C * k, C * k + 128, V("ZT", 0, 512))
    ts(V("NQ"), V("NBI"), 0.0125, MUL, -0.49375, ADD)
    cp(V("NQI"), V("NQ"))
    ts(V("NQ2"), V("NQI"), -79.75, MUL)
    tt(V("POS"), V("NBI"), V("NQ2"), ADD)

    def step(parts, A, G, K, w, tab, lst, scale, o0, o1, before=None, after=None):
        def gat(q, e, a, b):
            o, i = V(G, 16 * w * a + e, 16 * w * b, w), IND(tab, V(lst, 20 * e + a, 20 * e + b))
            if scale is None:
                move(q, o, i)
            else:
                aff(q, o, i, scale, 0.0)
        for a, b, nv in parts:
            for e in range(nv, 4):
                gat(FREE[0], e, a, b)
            if before is not None:
                before(a, b)
        for a, b, nv in parts:
            for e in range(nv):
                gat(FREE[1], e, a, b)
            scan(V(K, 16 * w * a, 16 * w * b), V(A, 16 * w * a, 16 * w * b), V(G, 16 * w * a, 16 * w * b), 0.0, o0, o1)
            if after is not None:
                after(a, b)

    def own_keys(a, b):
        scan(V("HOR", a, b), V("Z16", a, b), V("K4", 7 * a + 6, 7 * b, 7), 0.0, MUL, MAX)

    def signs(m, a, b, acc):
        act(V("JK", C * m + a, C * m + b), V("K4", 7 * a + 5, 7 * b, 7), AF.Sign, bias=col("HOR", 16 * m + 15), scale=-1.0, accum=col(acc, m))

    def count_early(a, b):
        if a == 0:
            own_keys(0, 16 * b)
            for m in range(NE):
                signs(m, 0, 16 * b, "P2")

    def count_pass(at):
        kr, h = V("K4", 5, 7 * C, 7), 16 * PARTS4[0][1]
        own_keys(h, C)
        for m in range(NH, NA):
            signs(m, h if m < NE else 0, C, "PL")
        if NH:
            n = C - h
            for m in range(NH):
                ts(V("CMH", n * m, n * m + n), V("K4", 7 * h + 5, 7 * C, 7), col("HOR", 16 * m + 15), LT)
            scan(V("CMG", 0, n * NH), V("APH", 0, n * NH), V("CMH", 0, n * NH), 0.0, MIN, ADD)
            ts(V("PL", 0, NH), V("CMG", n - 1, n * NH, n), 2.0, MUL, -float(n), ADD)
        for i in range(ND):
            ts(V("CMP", C * i, C * i + C), kr, col("HOR", 16 * (NA + i) + 15), LT)
        scan(V("CMS"), V("APS"), V("CMP"), 0.0, MIN, ADD)
        tt(V("PL", 0, NE), V("PL", 0, NE), V("P2", 0, NE), ADD)
        ts(V("CW", at + NA, at + 20), V("CMS", C - 1, C * ND, C), 160.0, ADD)
        ts(V("CW", at, at + NA), V("PL", 0, NA), 0.5, MUL, 159.5, ADD)

    def evac(b, pb, dst, d0, n, relu):
        o, i = V(dst, 4 * d0 + b, 4 * (d0 + n), 4), V("ps%d" % pb, 0, n)
        if EVAC[b] == "e" and relu:
            either(o, i, lambda: g.scalar.activation(o[0], i[0], AF.Relu, scale=0.03125),
                   lambda: g.vector.tensor_scalar(o[0], i[0], 0.0, 0.03125, MAX, MUL), i[1])
        elif EVAC[b] == "e":
            aff("e", o, i, 0.5, 0.0)
        elif EVAC[b] == "a":
            act(o, i, AF.Relu if relu else AF.Identity, scale=0.03125 if relu else 0.5)
        elif relu:
            ts(o, i, 0.0, MAX, 0.03125, MUL)
        else:
            ts(o, i, 0.5, MUL)

    def names_of(e):
        move("a", V("RR", C * e, C * e + C), IND(V("CN"), V("N1", 20 * e, 20 * e + 20)))

    def names_out(q, e):
        move(q, V("ONB", e, 4 * C, 4), IND(V("RR", C * e, C * e + C), V("OP")))

    def unplaced(cw):
        aff("a", V("G4", 5, 7 * C, 7), IND(V("T3"), cw), -2.0 ** -111, 832.0 * 2.0 ** -111)

    def pack(cw):
        for a, b in ((0, 10), (10, 20)):
            tt(V("PK", 16 * a, 16 * b), IND(V("T4K"), V("CW", cw + a, cw + b)), V("T3", 16 * a, 16 * b), ADD)

    def slot(i, a, b=C):
        return V("CT", 4 * (C * (i // 4) + a) + i % 4, 4 * (C * (i // 4) + b), 4)

    def compare(lo, hi, pb):
        pv, pa = "ps%d" % pb, "ps%d" % (pb + 1)
        narrow = lo == 0 and AHEAD and hi <= 128 and "v" not in RUNS[:hi // 16 - 1]
        mm(pb, "QU2", "SU2", 0, "QX", "SX", lo, 128 if narrow else C)
        mm(pb + 1, "QU2", "SU2", 0, "QX", "SX", lo, C)
        tt(V("M3", lo, hi), V(pv, 0, hi - lo), V("LM", lo, hi), MAX)
        scan(V("H3", lo, hi), V("A3", lo, hi), V("M3", lo, hi), 0.0, ADD, MIN)
        if lo == 0 and not AHEAD:
            scan(V("RM"), V(pv, 0, C), V("ONE", 0, C), -BIG, MAX, MUL)
            act(V("JK", 0, C), V("RM"), AF.Sign, bias=col("RM", C - 1), scale=-1.0, accum=CST)
            cp(col("OS", 0), CST)
        if lo == STAGES[-1][1] and AHEAD:
            scan(V("RM", lo, C), V(pv, 0, C - lo), V("ONE", lo, C), -BIG, MAX, MUL)
            act(V("JK", lo, C), V("RM", lo, C), AF.Sign, bias=col("RM", C - 1), scale=-1.0, accum=CUP)
        if lo == 0 and AHEAD:
            scan(V("RM", 0, hi), V(pv, 0, hi), V("ONE", 0, hi), -BIG, MAX, MUL)
            ts(TOPS, col("RM", hi - 1), col("RM", C - 1), MAX)
            act(V("JK", 0, hi), V("RM", 0, hi), AF.Sign, bias=TOPS, scale=-1.0, accum=CST)
            ts(CAD, CST, float(hi), EQ, CUP, MUL)
            ts(col("OS", 0), CST, CAD, ADD)
        tt(slot(0, lo, hi), V(pv, 0, hi - lo), V("H3", lo, hi), GT)
        for m in range(lo // 16, min(hi // 16, 19)):
            a, own = 16 * m + 16, col("H3", 16 * m + 15)
            if RUNS[m] == "a":
                act(V("SG", C * m + a, C * m + C), V(pa, a - lo, C - lo), AF.Sign, bias=own, scale=-1.0)
                act(slot(m + 1, a), V("SG", C * m + a, C * m + C), AF.Relu, scale=-1.0, accum=col("RS", m))
            else:
                ts(slot(m + 1, a), V("ps%d" % STAGES[-2][2], 0, C - a) if narrow else V(pv, a - lo, C - lo), own, GT)
                scan(V("RO", 20 * a + m, 20 * C, 20), V("ONE", a, C), slot(m + 1, a), col("CNT", m)[0], MUL, ADD, col("CNT", m))

    for stage in STAGES[:-1]:
        compare(*stage)
    for r in range(ROUNDS):
        last = r == ROUNDS - 1
        cw, cwn, qt, st = V("CW", 20 * r, 20 * r + 20), V("CW", 20 * r + 20, 20 * r + 40), "QT%d" % r, "STT%d" % r
        compare(*STAGES[-1])
        if r == 0:
            quant("QB", "SB", 0, 128, V("BL2"))
            for e in range(4):
                ts(V("NALL", e, 100, 5), V("POS", 20 * e, 20 * e + 20), 4.0, MUL)
        ts(V("D16"), IND(V("LR"), col("OS", 0)), 2.0 ** 35, ADD, 2.0 ** 35, SUB)
        ts(V("ST"), IND(V("LR"), col("OS", 0)), col("D16", 0), SUB)
        ts(V("EQ"), V("NALL"), col("ST", 0), EQ)
        scan(V("EQS"), V("EQ"), V("M5"), 0.0, MAX, MUL)
        ts(V("O1"), V("EQS", 4, 100, 5), 1.0, ADD)
        for (a, b), q in zip(SPLIT[len(Q_NF)], Q_NF):
            move(q, V("NFF", 16 * a, 16 * b), IND(V("FT", 0, 2), V("O1", a, b)))
        for (a, b), q in zip(SPLIT[len(Q_NF)], Q_NF):
            move(q, V("NFC", 16 * a, 16 * b), IND(V("NFF"), V("OP", a, b)))
        for k in TILES:
            quant("QC", "SQC", C * k + Q0[k], C * k + C, V("CT", 4 * (C * k + Q0[k]), 4 * (C * k + C)))
            mm(4, "QB", "SB", 0, "QC", "SQC", C * k, C * k + C, k == TILES[0], k == TILES[-1])
        scan(V("RD"), V("T16B"), slot(0, 0), 0.0, MIN, ADD)
        tt(V("UT"), V("RO", 20 * C - 20, 20 * C), V("RD", 15, C, 16), ADD)
        tt(V("UT"), V("UT"), V("RS"), ADD)
        if r == 0:
            move("a", V("HHB"), V("HH"))
        ts(V("US"), V("UT"), 160.0, ADD, SC, MUL)
        scan(V("HC"), V("HH"), V("ps4", 0, C), 0.0, MUL, ADD)
        tt(V("UB"), V("US"), V("HC", 15, C, 16), SUB)
        ts(V("BC"), V("UB"), ISC, MUL)
        scatter(V("SF", 16, 336), V("BC"), V("NFC"))
        aff("a", V("BYC"), IND(V("T3"), V("BC")), 1.0, -160.0)
        move("a", V("BYF"), IND(V("BYC"), cw))
        scan(V("HB"), V("HHB"), V("BYF"), 0.0, MUL, ADD)
        aff(Q_SD, V("SD"), V("SF", 15, 335), -1.0 - EPS, 1.0)
        ts(V("BF"), V("HB", 15, C, 16), ISC, MUL, 160.0, ADD)
        scan(V("K1S"), V("SD"), V("SF", 16, 336), -161.0, ADD, ADD)
        scan(V("D0S"), V("SF", 16, 336), V("ONE", 0, C), -160.0 * INF, ADD, MUL)
        for (a, b), q in zip(SPLIT[len(Q_K1)], Q_K1):
            aff(q, V("K1", 16 * a, 16 * b), IND(V("K1S"), V("BF", a, b)), 1.0, 161.0)
        act(T1, col("D0S", C - 1), AF.Relu, scale=EPS, bias=96.0)
        aff("e", RR_, T1, 1.0, 64.0)
        for (a, b), q in zip(SPLIT[len(Q_AA)], Q_AA):
            aff(q, V("AA", 80 * a + 4, 80 * b, 5), IND(V("D0S"), V("BF", a, b)), EPS, 480.0)
        aff(Q_R, NEGA, T1, -1.01 * EPS, -78.64 * EPS)
        aff(Q_R, S3, T1, -EPS, -68.0 * EPS)
        aff(Q_R, B3, T1, 320.0 * EPS, 1.0 + 320.0 * 68.0 * EPS)
        if r == 0:
            ts(V("N1"), V("POS"), 4.0, MUL)

        def cap(a, b):
            move("e", V("G", 80 * a + 4, 80 * b, 5), V("K1", 16 * a, 16 * b))
        step(PARTS, "AA", "G", "K2", 5, V("K1"), "N1", RR_, ADD, MIN, before=cap)
        for a, b in HALVES:
            aff("a", V("F3", 16 * a, 16 * b), V("AA", 80 * a + 4, 80 * b, 5), S3, B3)
            aff("a", V("AB", 112 * a + 4, 112 * b, 7), V("AA", 80 * a + 4, 80 * b, 5), -EPS, 1.0 + 320.0 * EPS)
        if r == 0:
            ts(V("N5"), V("POS"), 20.0, MUL, 4.0, ADD)
            unplaced(cw)

        def spread(a, b):
            act(V("EX", 16 * a, 16 * b), V("K3", 80 * a + 3, 80 * b, 5), AF.Exp, scale=NEGA, bias=TOP)
        step(PARTS3, "AA", "G", "K3", 5, V("K2"), "N5", RR_, ADD, MIN, after=spread)
        for a, b, _ in PARTS3:
            tt(V("E3", 16 * a, 16 * b), V("EX", 16 * a, 16 * b), V("F3", 16 * a, 16 * b), MUL)
        for a, b in HALVES:
            act(V("G4", 112 * a + 4, 112 * b, 7), V("K3", 80 * a + 4, 80 * b, 5), AF.Relu, scale=-2.0 ** 89, bias=CAPB)
        step(PARTS4, "AB", "G4", "K4", 7, V("E3"), "N1", None, MUL, MAX, after=count_early)
        count_pass(20 * r + 20)
        scatter(V("LR"), cwn, V("PK"))
        if last:
            move("a", V("CN"), IND(V("T3"), cwn))
            for e in range(2):
                names_of(e)
        else:
            unplaced(cwn)
        scan(V("HL"), V("HH"), V("LR"), 0.0, MUL, ADD)
        order = (1, 0, 3, 2)

        def take(t, a, b):
            move(TAKE[t], V("TT", 4 * a + t, 4 * b, 4), IND(xw, V("OT", 20 * t + a // 16, 20 * t + b // 16)))
        for t in order:
            ts(V("OT", 20 * t, 20 * t + 20), V("HL", 15, C, 16), ISC4, MUL, float(t), ADD)
        for a, b in TAKES:
            for t in order:
                take(t, a, b)
            top = max(b, a + 128)
            quant(qt, st, KB + a, KB + top, V("TT", 4 * a, 4 * top))
            if b == C:
                send(r)
        ts(V("VI"), V("HL", 15, C, 16), ISC, MUL)
        ts(V("HI"), V("VI"), 4095, AND)
        cp(V("OP"), V("HI"))
        if last:
            for e in (2, 3):
                names_of(e)
            for e in range(4):
                names_out("e", e)
            dma("s", T.on[:, :], T.ONB[0:128:16, :], V("ONB")[1], [])
            quant("QV", "SV", 0, 128, V("Vb"))
        else:
            pack(20 * r + 20)
        for lo, hi, pb, sb in PIECES:
            top = max(hi, lo + 128)
            for b in range(4):
                mm(pb + b, "QE", "SE", 128 * b, qt, st, KB + lo, KB + top, True, False)
                mm(pb + b, "QE", "SE", 128 * b, qt, st, lo, top, False, True)
            for b in range(4):
                evac(b, pb + b, "ZS", lo, hi - lo, False)
            quant("QZ", "SZ", lo, top, V("ZS", 4 * lo, 4 * top))
            for b in range(4):
                mm(pb + b, "QW", "SW", 128 * b, "QZ", "SZ", lo, top)
            for b in range(4):
                evac(b, pb + b, "XS", lo, hi - lo, True)
            quant("QX", "SX", lo, top, V("XS", 4 * lo, 4 * top))
            if last:
                mm(sb, "QV", "SV", 0, "QX", "SX", lo, top)
                dma("s", T.oc[:, 4 * lo:4 * hi], bits(V("QX", lo, hi)), V("QX", lo, hi)[1], [])
                move("e", V("YS", lo, hi), V("ps%d" % sb, 0, hi - lo))
                dma("s", T.y[:, lo:hi], V("YS", lo, hi)[0], V("YS", lo, hi)[1], [])
            else:
                for stage in STAGES[:-1]:
                    if stage[0] == lo:
                        compare(*stage)
    for k in range(4):
        dma("s" if k % 2 else "a", T.osc[4 * k:4 * k + 4, :], T.SX[32 * k:32 * k + 4, 0:C], V("SX")[1], [])
    issue()
    for sem in sorted(count):
        need("g", sem, count[sem])
    g.wait_ge(T.sem.sent, 2 * neng * ROUNDS)
